import numpy as np, ml_dtypes
CORES = [24,25,26,27,28,29,30,31]
N = 8
BF = ml_dtypes.bfloat16
def gentries(a):
    return np.ascontiguousarray(a.reshape(8, 16, -1).transpose(0, 2, 1)).reshape(8, -1)
def gtable(e):
    e = np.asarray(e); return np.ascontiguousarray(e.reshape(8, -1, 16).transpose(0, 2, 1)).reshape(128, -1).astype(np.int32)
P, C, CAP, TH, DAYS, BITS = 512, 8, 192, 960, 3, 11
W = N * P; M = 2 ** BITS; B0 = TH // 16; DEC = 8; STEP = 77
def parts(rng):
    x = (rng.random((N, 8, 16, P)) * B0 * rng.random((N, 8, 1, P))).astype(np.int64); x = np.minimum(x, B0 - 1)
    return x, rng.integers(0, W, (N, 8, C * P)), rng.integers(0, M, (N, 8, C * P)), rng.integers(0, 256, (N, 8, P))
def even(rng):
    u = rng.integers(-B0, B0 + 1, (N, 8, 8, P)); u[:, :, 0] = np.abs(u[:, :, 0])
    return np.concatenate([B0 + u, B0 - u], axis=2)
def sick(rng):
    e = even(rng)
    return np.minimum(e + ((256 - e) * rng.random((N, 8, 1, P)) * rng.random(e.shape)).astype(np.int64), 255)
def lean(rng):
    n = rng.integers(-(-TH // 255), 9, (N, 8, 1, P)); s = rng.integers(0, 16, (N, 8, 1, P)); lo = -(-TH // n)
    on = (np.arange(16)[:, None] - s) % 16 < n
    return np.where(on, np.minimum(lo + ((256 - lo) * rng.random((N, 8, 16, P))).astype(np.int64), 255), 0)
def mark(rng, x, share):
    return np.where(rng.random((N, 8, 1, P)) < share, sick(rng), x)
def pack(x, nb, dice, res):
    return {"x0": np.ascontiguousarray(x.reshape(N, 128, P)).astype(np.int32), "nb": np.stack([gtable(v) for v in nb]), "dice": np.stack([gtable(v) for v in dice]), "res": np.ascontiguousarray(res).astype(np.int32)}
def setup_inputs(rng):
    x, nb, dice, res = parts(rng); share = rng.choice(np.array([0.04, 0.1, 0.2, 0.45]), (N, 8, 1, 1))
    return pack(mark(rng, x, share), nb, dice, res)
def setup_inputs_room(rng):
    x, nb, dice, res = parts(rng); m = np.zeros((N, 8, P), bool)
    n = rng.choice(np.array([0, 1, CAP - 1, CAP, CAP + 1, P]), (N, 8))
    n[0] = (CAP, CAP + 1, P, CAP - 1, 1, 0, CAP, CAP + 1)
    n[1] = (0, P, CAP + 1, 1, CAP - 1, CAP, CAP, CAP)
    n[2] = (CAP, CAP + 1, CAP, P, CAP, CAP + 1, CAP, CAP)
    n[3, ::2] = CAP
    j = P - CAP; cnt = W - int(np.sum(np.minimum(n[:, 6], CAP)))
    while -(-j * M // cnt) * cnt >= (j + 1) * M: j += 1; cnt += 1
    n[0, 6] = P - j; d = -(-j * M // cnt)
    for q in range(N):
        for g in range(8):
            o = rng.permutation(P)
            if (q == 0 and g >= 6) or (q == 1 and g == 7): o = np.arange(P)[::-1]
            if (q == 1 and g == 6) or (q == 2 and g == 7): o = np.arange(P)
            if q == 3: o = np.argsort(rng.permutation(16)[np.arange(P) % 16], kind="stable")
            m[q, g, o[:int(n[q, g])]] = True
    x = np.where(m[:, :, None, :], sick(rng), x)
    x[:, 6] = np.where(m[:, 6][:, None, :], even(rng)[:, 6], x[:, 6]); res[:, 6] = 255
    dice[:, 6] = np.where(rng.random((N, C * P)) < 0.1, d, dice[:, 6])
    return pack(x, nb, dice, res)
def setup_inputs_ties(rng):
    x, nb, dice, res = parts(rng)
    x = np.where(rng.random((N, 8, 1, P)) < 0.2, rng.choice(np.array([0, 7, 8, 9]), x.shape), x)
    x = mark(rng, x, 0.06); e = even(rng); e[:, :, 0] += rng.integers(-1, 2, (N, 8, P))
    x = np.where(rng.random((N, 8, 1, P)) < 0.35, e, x)
    x = np.where(rng.random((N, 8, 1, P)) < 0.08, lean(rng), x)
    res = np.where(rng.random(res.shape) < 0.7, rng.choice(np.array([0, 1, 7, 8, 9, 255]), res.shape), res)
    return pack(x, nb, dice, res)
def setup_inputs_ends(rng):
    x, nb, dice, res = parts(rng); x = mark(rng, x, 0.15); s = sick(rng)
    x[..., 0] = s[..., 0]; x[..., P - 1] = s[..., P - 1]
    nb[:, 1::2] = np.tile(nb[:, 1::2, :P], (1, 1, C))
    nb[:, 2] = rng.choice(np.array([0, P - 1, W - P, W - 1]), (N, C * P))
    nb[:, 4] = P * np.arange(N)[:, None] + rng.integers(0, P, (N, C * P))
    me = P * np.arange(N)[:, None] + np.tile(np.arange(P), C)[None, :]
    nb[:, 6] = np.where(rng.random((N, C * P)) < 0.5, me, nb[:, 6])
    dice = np.where(rng.random(dice.shape) < 0.8, rng.choice(np.array([0, 1, M - 1, M - 2, M - STEP, M - STEP - 1, M - 2 * STEP, M // 2]), dice.shape), dice)
    return pack(x, nb, dice, res)
def setup_inputs_cold(rng):
    x, nb, dice, res = parts(rng); share = rng.choice(np.array([0.05, 0.15, 0.3]), (N, 8, 1, 1))
    q = rng.permutation(N); c = rng.permutation(8)
    share[q[0]] = 1.0; share[q[1]] = 0.0; share[:, c[0]] = 0.0; share[:, c[1]] = 1.0; share[:, c[[2, 4, 5]]] = 0.0
    x = mark(rng, x, share); e = even(rng)
    a, v = int(rng.integers(0, N)), int(rng.integers(0, P)); x[a, c[2], :, v] = 255
    late = rng.random((N, 1, P)) < 0.25; last = np.arange(C)[:, None] == C - 1
    nb[:, c[2]] = np.where((last | ~late).reshape(N, C * P), a * P + v, nb[:, c[2]])
    nb[q[1], c[3]] = q[0] * P + rng.integers(0, CAP, C * P)
    h = rng.random((N, 1, P)) < 0.2; stay = rng.random((N, 1, P)) < 0.5; stay[q[2]] = False
    x[:, c[4]] = np.where(h, np.where(stay, 255, e[:, c[4]]), x[:, c[4]]); res[:, c[4]] = 255
    h = rng.random((N, P)) < 0.1; u = np.arange(W).reshape(N, P)
    x[:, c[5]] = np.where(h[:, None, :], rng.integers(min(B0 + DEC * DAYS, 255), 256, (N, 16, P)), x[:, c[5]]); res[:, c[5]] = rng.integers(0, 32, (N, P))
    nb[:, c[5]] = np.where(np.tile(h, (1, C)), rng.choice(u[h], (N, C * P)), rng.choice(u[~h], (N, C * P)))
    return pack(x, nb, dice, res)
def setup_inputs_spread(rng):
    x, nb, dice, res = parts(rng)
    x = np.minimum((np.exp2(8 * rng.random((N, 8, 1, P))) * rng.random((N, 8, 16, P))).astype(np.int64), 255)
    res = np.minimum(np.exp2(8 * rng.random((N, 8, P))).astype(np.int64) - 1, 255)
    nb = np.minimum((W * rng.random((N, 8, C * P)) ** rng.choice(np.array([1, 2, 3]), (N, 8, 1))).astype(np.int64), W - 1)
    dice = np.minimum((M * rng.random((N, 8, C * P)) ** 2).astype(np.int64), M - 1)
    return pack(x, nb, dice, res)
def check_inputs(d):
    bad = []
    for k, hi in (("x0", 255), ("nb", W - 1), ("dice", M - 1), ("res", 255)):
        if np.min(d[k]) < 0 or np.max(d[k]) > hi: bad.append("range of " + k)
    return bad
def reference(x0, nb, dice, res):
    x = x0.astype(np.int64).reshape(N, 8, 16, P); r = res.astype(np.int64).reshape(N, 8, 1, P)
    link = np.stack([gentries(v) for v in nb]).astype(np.int64); dr = np.stack([gentries(v) for v in dice]).astype(np.int64)
    for t in range(DAYS):
        high = (np.add.reduce(x, axis=2) >= TH).astype(np.int64); before = np.add.accumulate(high, axis=2) - high
        ill = (high == 1) & (before < CAP)
        flag = np.ascontiguousarray(ill.transpose(1, 0, 2)).reshape(8, W)
        win = np.ascontiguousarray(np.where(ill[:, :, None, :], x, 0).transpose(1, 2, 0, 3)).reshape(8, 16, W)
        come = []
        for q in range(N):
            come.append(np.maximum.reduce(np.take_along_axis(win, link[q][:, None, :], 2).reshape(8, 16, C, P), axis=2))
        d = (dr + STEP * t) & (M - 1); new = link.copy()
        for g in range(8):
            sl = np.flatnonzero(~flag[g])
            hit = flag[g][link[:, g]] & ~np.tile(ill[:, g], (1, C))
            new[:, g] = np.where(hit, sl[(d[:, g] * len(sl)) >> BITS], link[:, g])
        x = np.maximum(np.maximum(x - DEC, np.stack(come) - r), 0); link = new
    return {"yx": x.reshape(N, 128, P).astype(np.float32), "ynb": np.stack([gtable(v) for v in link]).astype(np.float32)}

@@ -1,0 +1,366 @@
+from concourse.bass import DstId, RemoteDMATransfer
+from concourse.mybir import AluOpType as A, ActivationFunctionType as AF
+
+P, NR, DAYS = 512, 8, 3
+WB = 520
+CAP, TH, STEP = 192, 960, 77
+
+
+def sb(cols, dtype):
+    return ("sbuf", [128, cols], dtype)
+
+
+BF, F32, I32, U16, F16 = "bfloat16", "float32", "int32", "uint16", "float16"
+SCRATCH = {
+    "xi": sb(512, I32), "nbi": sb(256, I32), "d0": sb(256, I32), "ri": sb(512, I32), "rb": sb(512, BF), "nx0": sb(512, BF),
+    "win0": sb(NR * WB, BF), "win1": sb(NR * WB, BF), "win2": sb(NR * WB, BF),
+    "ll0": sb(NR * P, BF), "ll1": sb(NR * P, BF), "ll2": sb(NR * P, BF),
+    "G": sb(4608, BF), "O": sb(4608, BF), "D0": sb(4608, BF), "SG": sb(4096, BF),
+    "ones": sb(128, BF), "B1": sb(128, BF), "B": sb(128, BF), "idb": sb(128, BF), "idh": sb(128, F16), "idf": sb(128, F32),
+    "E": sb(128, BF), "Z": sb(144, BF), "k2048": sb(128, BF),
+    "high": sb(512, BF), "cb": sb(1040, BF), "capa": sb(512, BF), "capb": sb(512, BF),
+    "pi": sb(8, I32), "pm": sb(8, I32), "pf": sb(8, F32), "i32": sb(32, I32), "vc": sb(32, F32),
+    "pa": sb(32, F32), "pb": sb(32, F32), "pc": sb(32, F32), "pos": sb(32, U16),
+    "iw0": sb(32, BF), "iw1": sb(32, BF), "iw2": sb(32, BF),
+    "k512": sb(8, F32), "C": sb(8, F32), "cs": sb(8, F32), "nf": sb(8, F32),
+    "t1": sb(256, I32), "t2": sb(256, F32), "t3": sb(256, I32), "d1": sb(256, I32), "d2": sb(256, I32),
+    "L": sb(256, F32), "off": sb(256, U16), "ju": sb(256, U16), "jh": sb(256, F16), "tm": sb(7 * 256, BF),
+    "idx": sb(256, U16), "h": sb(256, F32), "yxs": sb(512, F32), "ynbs": sb(256, F32),
+}
+for _n in ("pTa", "pTb", "pW", "pF", "pI", "pSa", "pSb", "pSc"):
+    SCRATCH[_n] = ("psum", [128, 512], F32)
+SEMAPHORES = ["cV", "cS", "cP", "cG", "ldxa", "ldxb", "ldn", "ldd", "ldr", "sty", "stn0", "stn1", "stn2", "sent",
+              "aw0", "aw1", "aw2", "al0", "al1", "al2"]
+
+CA = [12, 16, 16]
+VK = (1, 2)
+VKL = 2
+FPRE, FMID = 5, 2
+SLA = (128, 192)
+SLL = (112, 192, 224)
+
+
+def rank_program(g, core, T, topo):
+    q = T.rank_of(core)
+    if q is None:
+        return
+    V, S, PE, SY = g.vector, g.scalar, g.tensor, g.sync
+    Q = {"V": V, "S": S, "P": PE, "G": g, "Y": SY}
+    count = {"cV": 0, "cS": 0, "cP": 0, "cG": 0}
+    known = {k: {} for k in Q}
+    writer, readers = {}, {}
+
+    def need(e, ev):
+        sem, val, clock = ev
+        if known[e].get(sem, 0) < val:
+            Q[e].wait_ge(T.sem[sem], val)
+            known[e][sem] = val
+        for s, v in clock.items():
+            if known[e].get(s, 0) < v:
+                known[e][s] = v
+
+    def op(e, fn, r=(), w=(), x=(), sem=None):
+        evs = [writer[k][1] for k in tuple(r) + tuple(w) if k in writer]
+        evs += [ev for k in w for qe, ev in readers.get(k, [])]
+        evs += [writer[k][1] for k in x if k in writer and writer[k][0] != e]
+        for ev in sorted(evs, key=lambda z: -z[1]):
+            need(e, ev)
+        ins = fn()
+        if sem is None:
+            sem = "c" + e
+            count[sem] += 1
+            ins.then_inc(T.sem[sem], 1)
+            ev = (sem, count[sem], dict(known[e]))
+        else:
+            ins.then_inc(T.sem[sem], 16)
+            ev = (sem, 16, dict(known[e]))
+            e = "dma"
+        for k in r:
+            readers.setdefault(k, []).append((e, ev))
+        for k in tuple(w) + tuple(x):
+            writer[k] = (e, ev)
+            readers[k] = []
+
+    def ts(out, in0, s1, s2, o0, o1=None):
+        if o1 is None:
+            return V.tensor_scalar(out, in0, s1, None, o0)
+        return V.tensor_scalar(out, in0, s1, s2, o0, o1)
+
+    def group(mms, start=True, stop=True):
+        ins = None
+        for i, (o, l, rr) in enumerate(mms):
+            ins = PE.matmul(o, l, rr, start and i == 0, stop and i == len(mms) - 1)
+        return ins
+
+    others = [T.cores[(q + i) % NR] for i in range(1, NR)]
+    others.sort(key=lambda c: topo.die(c) == topo.die(core))
+    emask = -1
+    for c in others:
+        emask &= topo.mask(core, c)
+    neng = bin(emask).count("1")
+    sent = {"sent": 0}
+
+    def allgather(ap, r, sem, name):
+        for k in r:
+            need("G", writer[k][1])
+        ids = [DstId(rid=topo.addr(c)[0], pnc=topo.addr(c)[1]) for c in others]
+        g.remote_dma_fused([RemoteDMATransfer(dst_ids=ids, dma_engine_mask=emask, remote_sem=T.sem[sem], src=ap,
+                                              dsts=[ap for _ in others])], local_sem=T.sem.sent)
+        sent["sent"] += neng
+        sent[sem] = sent.get(sem, 0) + neng * (NR - 1)
+        writer[name] = ("dma", (sem, sent[sem], {}))
+
+    win = [T.win0, T.win1, T.win2]
+    ll = [T.ll0, T.ll1, T.ll2]
+    dd = [T.d0, T.d1, T.d2]
+    iw = [T.iw0, T.iw1, T.iw2]
+    Wr = [T.Z[:, 15 - r:143 - r] for r in range(16)]
+    cq = T.cb[:, 16:528]
+    va = 16 * CA[0]
+
+    op("Y", lambda: SY.dma_start(T.xi[:, 0:va], T.x0[:, 0:va]), w=["xia"], sem="ldxa")
+    op("S", lambda: S.dma_start(T.xi[:, va:P], T.x0[:, va:P]), w=["xib"], sem="ldxb")
+    op("Y", lambda: SY.dma_start(T.nbi[:], T.nb[:]), w=["nbi"], sem="ldn")
+    op("S", lambda: S.dma_start(T.ri[0:8, :], T.res[:]), w=["ri"], sem="ldr")
+    op("Y", lambda: SY.dma_start(T.d0[:], T.dice[:]), w=["d0"], sem="ldd")
+    op("V", lambda: V.memset(T.ones[:], 1.0), w=["ones"])
+    op("V", lambda: V.memset(T.D0[:, 0:576], 0.0), w=["D0a"])
+    op("V", lambda: V.memset(T.capa[:], float(CAP + 8 * q)), w=["capa"])
+    op("V", lambda: V.memset(T.cb[:, 0:16], float(8 * q)), w=["c0"])
+    op("V", lambda: V.memset(T.D0[:, 0:576:9], 512.0), r=["D0a"], w=["D0a"])
+    op("V", lambda: V.memset(T.Z[:], 0.0), w=["Z"])
+    op("V", lambda: V.memset(T.k512[:], float(P)), w=["k512"])
+    op("V", lambda: V.memset(T.capb[:], float(CAP)), w=["capb"])
+    op("V", lambda: V.memset(T.k2048[:], 2048.0), w=["k2048"])
+    op("G", lambda: g.affine_select(T.B1[:], T.ones[:], [[-16, 8], [0, 16]], A.is_ge, 0.0, 0, 1), r=["ones"], w=["B1"])
+    op("G", lambda: g.affine_select(T.B[:], T.B1[:], [[16, 8], [0, 16]], A.is_ge, 0.0, 15, -1), r=["B1"], w=["B"])
+    op("G", lambda: g.iota(T.pi[:], [[0, 8]], 0, 1), w=["pi"])
+    op("G", lambda: g.iota(T.i32[:], [[16, 32]], 0, 0), w=["i32"])
+    op("G", lambda: g.affine_select(T.idb[:], T.ones[:], [[-1, 128]], A.is_equal, 0.0, 0, 1), r=["ones"], w=["idb"])
+    op("G", lambda: g.affine_select(T.E[0:8, :], T.ones[0:8, :], [[-1, 8], [0, 16]], A.is_equal, 0.0, 0, 1), r=["ones"], w=["E"])
+    for n in (576, 1152, 2304):
+        op("S", lambda: S.activation(T.D0[:, n:2 * n], T.D0[:, 0:n], AF.Copy), r=["D0a"], w=["D0a"])
+    op("V", lambda: ts(T.pm[:, 0:1], T.pi[:, 0:1], 15, None, A.bitwise_and), r=["pi"], w=["pm0"])
+    op("V", lambda: ts(T.Z[:, 15:128:16], T.B[:, 0:128:16], 1.0 / 16, None, A.mult), r=["B", "Z"], w=["Z"])
+    op("V", lambda: V.tensor_copy(T.pf[:, 0:1], T.pm[:, 0:1]), r=["pm0"], w=["pf0"])
+    op("V", lambda: ts(T.vc[:], T.i32[:], T.pf[:, 0:1], None, A.add), r=["pf0", "i32"], w=["vc"])
+
+    def flags(t, ks):
+        for k in ks:
+            out = T.pF[:, 32 * k:32 * k + 32]
+            mm = [(out, Wr[r], T.G[:, 9 * r + k::144]) for r in range(16)] + [(out, T.idb[:], iw[t][:])]
+            op("P", lambda: group(mm), r=["Z", "idb", "iw%d" % t, "Ga%d" % k, "Gb%d" % k], x=["pF"])
+
+    def total(h, v0, v1, nx):
+        op("P", lambda: PE.matmul(T["pT" + h][:, 0:v1 - v0], T.B[:], nx(v0, v1), True, True), r=["B", "nx" + h], x=["pT" + h])
+
+    def infect(t, h, v0, v1, nx):
+        qo = 8 * q if t < DAYS - 1 else 0
+        cap = T.capa if t < DAYS - 1 else T.capb
+        c, cp, il = T.cb[:, 16 + v0:16 + v1], T.cb[:, 15 + v0:15 + v1], T.cb[:, 528 + v0:528 + v1]
+        prev = "c0" if h == "a" else "cqa"
+        op("V", lambda: ts(T.high[:, v0:v1], T["pT" + h][:, 0:v1 - v0], -TH + 0.5, None, A.is_le), w=["high" + h], x=["pT" + h])
+        op("V", lambda: V.tensor_tensor_scan(c, T.high[:, v0:v1], cap[:, v0:v1], T.cb[:, 15 + v0:16 + v0], A.add, A.min),
+           r=["high" + h, "capa", "capb", prev], w=["cq" + h])
+        op("V", lambda: V.tensor_tensor_scan(il, c, cp, 0.0, A.max, A.subtract), r=["cq" + h, prev], w=["ill" + h])
+        names = ["blk%d%s" % (t, h)]
+        if h == "b":
+            op("V", lambda: ts(win[t][:, WB * q + P:WB * (q + 1)], T.cb[:, 520:528], float(-qo), None, A.add), r=["cqb"], w=["tail%d" % t])
+            names.append("tail%d" % t)
+        op("V", lambda: V.tensor_tensor_scan(win[t][:, WB * q + v0:WB * q + v1], il, nx(v0, v1), 0.0, A.max, A.mult),
+           r=["ill" + h, "nx" + h], w=names[:1])
+        allgather(win[t][:, WB * q + v0:WB * q + (v1 if h == "a" else WB)], names, "aw%d" % t, "win%d" % t)
+
+    def uninfected(t, nx):
+        qo = 8 * q if t < DAYS - 1 else 0
+        op("P", lambda: group([(T.pW[:, 0:64], Wr[r], T.cb[:, 16 + r:1040:16]) for r in range(16)]),
+           r=["Z", "cqa", "cqb", "illa", "illb"], x=["pW"])
+        op("V", lambda: ts(T.G[:, 8::9], nx(0, P), 8.0, 0.0, A.add, A.min), r=["nxa", "nxb"], w=["G8"])
+        op("V", lambda: ts(T.pa[:], T.pW[:, 32:64], 1024.0, -512.0, A.mult, A.add), w=["pa"], x=["pW"])
+        op("V", lambda: ts(iw[t][:], T.pW[:, 32:64], 512.0, None, A.mult), w=["iw%d" % t], x=["pW"])
+        op("V", lambda: V.tensor_tensor(T.pb[:], T.pa[:], T.vc[:], A.max), r=["pa", "vc"], w=["pb"])
+        op("V", lambda: V.tensor_tensor(T.pc[:], T.pb[:], T.pW[:, 0:32], A.subtract), r=["pb"], w=["pc"], x=["pW"])
+        op("V", lambda: ts(T.pos[:], T.pc[:], float(qo), None, A.add), r=["pc"], w=["pos"])
+        lb = ll[t][:, P * q:P * (q + 1)]
+        op("V", lambda: V.tensor_copy(lb.indirect(T.pos[:]), cq), r=["pos", "cqa", "cqb"], w=["lb%d" % t])
+        allgather(lb, ["lb%d" % t], "al%d" % t, "ll%d" % t)
+
+    def nx0(v0, v1):
+        return T.nx0[:, v0:v1]
+
+    def nxo(v0, v1):
+        return T.O[:, 9 * v0 + 8:9 * v1:9]
+
+    LN = ["L0", "L1", "L2"]
+    op("V", lambda: ts(T.nx0[:, 0:va], T.xi[:, 0:va], -1.0, None, A.mult), r=["xia"], w=["nxa"])
+    total("a", 0, va, nx0)
+    op("V", lambda: ts(T.nx0[:, va:P], T.xi[:, va:P], -1.0, None, A.mult), r=["xib"], w=["nxb"])
+    total("b", va, P, nx0)
+    infect(0, "a", 0, va, nx0)
+    infect(0, "b", va, P, nx0)
+    uninfected(0, nx0)
+    op("V", lambda: V.tensor_copy(T.rb[0:8, :], T.ri[0:8, :]), r=["ri"], w=["rb"])
+    op("V", lambda: ts(T.t1[:], T.nbi[:], 3584, None, A.bitwise_and), r=["nbi"], w=["t1"])
+    op("P", lambda: PE.matmul(T.pTa[:], T.E[0:8, :], T.rb[0:8, :], True, True), r=["E", "rb"], x=["pTa"])
+    op("S", lambda: S.activation(T.D0[:, 8::9], T.pTa[:], AF.Copy), r=["D0a"], w=["D0a"], x=["pTa"])
+    op("V", lambda: ts(T.t3[:], T.d0[:], float(STEP), None, A.add), r=["d0"], w=["t3"])
+    op("V", lambda: ts(T.t2[:], T.t1[:], 1.0 / 64, -2048.0, A.mult, A.add), r=["t1"], w=["t2"])
+    op("V", lambda: ts(T.d1[:], T.t3[:], 2047, None, A.bitwise_and), r=["t3"], w=["d1"])
+    op("V", lambda: V.tensor_tensor(T.L[:], T.t2[:], T.nbi[:], A.add), r=["t2", "nbi"], w=LN)
+    op("V", lambda: V.tensor_copy(T.idh[:], T.idb[:]), r=["idb"], w=["idh"])
+    op("V", lambda: ts(T.off[:], T.L[:], 2048.0, None, A.add), r=LN, w=["off"])
+    op("V", lambda: ts(T.idf[:], T.idb[:], -1.0, None, A.mult), r=["idb"], w=["idf"])
+    op("V", lambda: ts(T.t3[:], T.d0[:], float(2 * STEP), None, A.add), r=["d0"], w=["t3"])
+    op("V", lambda: ts(T.d2[:], T.t3[:], 2047, None, A.bitwise_and), r=["t3"], w=["d2"])
+
+    def index_terms(out, a, b):
+        return [(out, T.idh[:], T.jh[:, a:b])] + [(out, T.idb[:], T.tm[:, 256 * i + a:256 * i + b]) for i in range(7)]
+
+    for t in range(DAYS):
+        last = t == DAYS - 1
+        wn = ["win%d" % t, "blk%da" % t, "blk%db" % t, "tail%d" % t]
+        w = win[t][:]
+        ln = ["ll%d" % t, "lb%d" % t, "idx"]
+        tmn = ["jh", "idh", "idb"] + ["tm%d" % i for i in range(7)]
+        bounds = (0,) + SLA + (256,) if not last else (0, SLL[0], SLL[1], 256)
+        banks = ["pSa", "pSb", "pSc"]
+
+        def pick(e, out, src, r, names):
+            if e == "V":
+                op("V", lambda: V.tensor_copy(out, src), r=r, w=names)
+            else:
+                op("S", lambda: S.activation(out, src, AF.Copy), r=r, w=names)
+
+        def gather(e, k, c0, c1, names):
+            pick(e, T.G[:, 144 * c0 + k:144 * c1:9], w.indirect(T.off[:, 32 * k + c0:32 * k + c1]), wn + ["off"], names)
+
+        def slg(e, c0, c1, name):
+            pick(e, T.SG[:, 16 * c0:16 * c1], ll[t][:].indirect(T.idx[:, c0:c1]), ln, [name])
+
+        def counts():
+            op("V", lambda: V.tensor_tensor_scan(T.C[:], T.k512[:], win[t][:, WB - 1::WB], 0.0, A.add, A.subtract), r=wn + ["k512"], w=["C"])
+            op("V", lambda: V.tensor_copy(T.nf[:], win[t][:, WB - 1::WB]), r=wn, w=["nf"])
+
+        def scale():
+            op("V", lambda: ts(T.cs[:, 0:1], T.C[:, 7:8], 1.0 / 2048, None, A.mult), r=["C"], w=["cs"])
+
+        def places():
+            op("V", lambda: ts(T.ju[:], dd[t][:], T.cs[:, 0:1], -0.5 + 2.0 ** -12, A.mult, A.add), r=["cs", "d%d" % t], w=["ju"])
+            op("V", lambda: ts(T.jh[:], T.ju[:], -2048.0, None, A.add), r=["ju"], w=["jh"])
+            for i in range(7):
+                op("V", lambda: ts(T.tm[:, 256 * i:256 * (i + 1)], T.ju[:], T.C[:, i:i + 1], T.nf[:, i:i + 1], A.is_ge, A.mult),
+                   r=["ju", "C", "nf"], w=["tm%d" % i])
+            op("P", lambda: group(index_terms(T.pI[:, 0:256], 0, 256)), r=tmn, x=["pI"])
+
+        def offsets():
+            op("V", lambda: ts(T.idx[:], T.pI[:, 0:256], 2048.0, None, A.add), w=["idx"], x=["pI"])
+
+        def update(v0, v1, hs):
+            op("V", lambda: V.tensor_tensor_scan(T.O[:, 9 * v0:9 * v1], T.D0[:, 9 * v0:9 * v1], T.G[:, 9 * v0:9 * v1], 0.0, A.add, A.min),
+               r=["G%s%d" % (h, k) for k in range(8) for h in hs] + ["G8", "D0a"], w=["nx" + h for h in hs])
+
+        def prewrap():
+            for i in range(3):
+                c0, c1 = bounds[i], bounds[i + 1]
+                out = T[banks[i]][:, 0:c1 - c0]
+                mm = index_terms(out, c0, c1) + [(out, T.idf[:], T.L[:, c0:c1])]
+                if last:
+                    mm.append((out, T.idb[:], T.k2048[:, 0:c1 - c0]))
+                op("P", lambda: group(mm, stop=False), r=tmn + LN + ["idf", "k2048"], x=[banks[i]])
+
+        def wrap(i, names):
+            c0, c1 = bounds[i], bounds[i + 1]
+            out = T[banks[i]][:, 0:c1 - c0]
+            op("P", lambda: group([(out, Wr[r], T.SG[:, 16 * c0 + r:16 * c1:16]) for r in range(16)], start=False), r=["Z"] + names, x=[banks[i]])
+
+        def select(i):
+            c0, c1 = bounds[i], bounds[i + 1]
+            dl = T.pW[:, 256 + c0:256 + c1]
+            op("V", lambda: V.tensor_tensor(dl, T[banks[i]][:, 0:c1 - c0], T.h[:, c0:c1], A.mult), r=["h"], w=["dl%d" % i], x=[banks[i], "pW"])
+            if last:
+                op("V", lambda: V.tensor_tensor(T.ynbs[:, c0:c1], dl, T.L[:, c0:c1], A.add), r=["dl%d" % i, LN[i]], w=["yn%d" % i], x=["pW"])
+                op("Y", lambda: SY.dma_start(T.ynb[:, c0:c1], T.ynbs[:, c0:c1]), r=["yn%d" % i], sem="stn%d" % i)
+            else:
+                op("V", lambda: V.tensor_tensor(T.L[:, c0:c1], dl, T.L[:, c0:c1], A.add), r=["dl%d" % i], w=[LN[i]], x=["pW"])
+
+        def hit():
+            op("V", lambda: ts(T.h[:], T.pF[:, 0:256], -30.0, None, A.is_lt), w=["h"], x=["pF"])
+
+        if not last:
+            ca = CA[t + 1]
+            va = 16 * ca
+            ka, kb = 8 - VK[0], 8 - VK[1]
+            for k in range(ka):
+                gather("S", k, 0, ca, ["Ga%d" % k])
+            for k in range(kb):
+                gather("S", k, ca, 32, ["Gb%d" % k])
+            counts()
+            both = list(range(ka, 8))
+            for k in both:
+                gather("V", k, 0, 32, ["Ga%d" % k, "Gb%d" % k])
+            scale()
+            for k in range(kb, ka):
+                gather("V", k, ca, 32, ["Gb%d" % k])
+            flags(t, both)
+            rest = list(range(kb, ka)) + list(range(kb))
+            places()
+            update(0, va, "a")
+            total("a", 0, va, nxo)
+            offsets()
+            if t == DAYS - 2:
+                op("V", lambda: V.memset(T.cb[:, 0:16], 0.0), w=["c0"])
+            infect(t + 1, "a", 0, va, nxo)
+            update(va, P, "b")
+            for i in range(3):
+                slg("S", bounds[i], bounds[i + 1], "SG%d" % i)
+            flags(t, rest[:FPRE])
+            total("b", va, P, nxo)
+            flags(t, rest[FPRE:FPRE + FMID])
+            infect(t + 1, "b", va, P, nxo)
+            uninfected(t + 1, nxo)
+            flags(t, rest[FPRE + FMID:])
+            prewrap()
+            for i in range(3):
+                wrap(i, ["SG%d" % i])
+            hit()
+            for i in range(3):
+                select(i)
+            op("V", lambda: ts(T.off[:], T.L[:], 2048.0, None, A.add), r=LN, w=["off"])
+        else:
+            ks = 8 - VKL
+            for k in range(ks):
+                gather("S", k, 0, 32, ["Ga%d" % k, "Gb%d" % k])
+            counts()
+            op("V", lambda: ts(T.t1[:], T.L[:], 1.0 / WB, 2048.0 / WB - 0.499, A.mult, A.add), r=LN, w=["t1"])
+            scale()
+            op("V", lambda: ts(T.t2[:], T.t1[:], -8.0, 2048.0, A.mult, A.add), r=["t1"], w=["t2"])
+            flags(t, [0, 1])
+            places()
+            op("V", lambda: V.tensor_tensor(T.L[:], T.L[:], T.t2[:], A.add), r=["t2"], w=LN)
+            gather("V", 7, 0, 32, ["Ga7", "Gb7"])
+            offsets()
+            for k in range(ks, 7):
+                gather("V", k, 0, 32, ["Ga%d" % k, "Gb%d" % k])
+            flags(t, [2, 3])
+            prewrap()
+            flags(t, [7, 4, 6, 5])
+            a, b, c = SLL
+            slg("S", 0, a, "SG0")
+            update(0, P, "ab")
+            slg("V", a, b, "SG1")
+            op("S", lambda: S.activation(T.yxs[:], T.O[:, 8::9], AF.Copy, scale=-1.0), r=["nxa", "nxb"], w=["yxs"])
+            op("Y", lambda: SY.dma_start(T.yx[:], T.yxs[:]), r=["yxs"], sem="sty")
+            slg("S", b, c, "SG2")
+            slg("V", c, 256, "SG3")
+            wrap(0, ["SG0"])
+            wrap(1, ["SG1"])
+            wrap(2, ["SG2", "SG3"])
+            hit()
+            for i in range(3):
+                select(i)
+
+    g.wait_ge(T.sem.sent, sent["sent"])
+    for s in ("cV", "cS", "cP", "cG"):
+        SY.wait_ge(T.sem[s], count[s])
+    for s in ("sty", "stn0", "stn1", "stn2"):
+        SY.wait_ge(T.sem[s], 16)

@@ -4,6 +4,7 @@ from concourse.mybir import AluOpType as A, ActivationFunctionType as AF
 P, NR, DAYS = 512, 8, 3
 WB = 520
 CAP, TH, STEP = 192, 960, 77
+UB = 136
 
 
 def sb(cols, dtype):
@@ -17,15 +18,16 @@ SCRATCH = {
     "ll0": sb(NR * P, BF), "ll1": sb(NR * P, BF), "ll2": sb(NR * P, BF),
     "G": sb(4608, BF), "O": sb(4608, BF), "D0": sb(4608, BF), "SG": sb(4096, BF),
     "ones": sb(128, BF), "B1": sb(128, BF), "B": sb(128, BF), "idb": sb(128, BF), "idh": sb(128, F16), "idf": sb(128, F32),
-    "E": sb(128, BF), "Z": sb(144, BF), "k2048": sb(128, BF),
+    "id8": sb(128, BF), "idm8": sb(128, BF), "idp": sb(128, F32),
+    "E": sb(128, BF), "Z": sb(144, BF), "kneg": sb(128, BF), "kpos": sb(128, BF),
     "high": sb(512, BF), "cb": sb(1040, BF), "capa": sb(512, BF), "capb": sb(512, BF),
     "pi": sb(8, I32), "pm": sb(8, I32), "pf": sb(8, F32), "i32": sb(32, I32), "vc": sb(32, F32),
     "pa": sb(32, F32), "pb": sb(32, F32), "pc": sb(32, F32), "pos": sb(32, U16),
     "iw0": sb(32, BF), "iw1": sb(32, BF), "iw2": sb(32, BF),
     "k512": sb(8, F32), "C": sb(8, F32), "cs": sb(8, F32), "nf": sb(8, F32),
-    "t1": sb(256, I32), "t2": sb(256, F32), "t3": sb(256, I32), "d1": sb(256, I32), "d2": sb(256, I32),
+    "t1": sb(256, I32), "t2": sb(256, F32), "t3": sb(256, I32), "t4": sb(256, I32), "d1": sb(256, I32), "d2": sb(256, I32),
     "L": sb(256, F32), "off": sb(256, U16), "ju": sb(256, U16), "jh": sb(256, F16), "tm": sb(7 * 256, BF),
-    "idx": sb(256, U16), "h": sb(256, F32), "yxs": sb(512, F32), "ynbs": sb(256, F32),
+    "idx": sb(256, U16), "h": sb(256, F32), "ub": sb(256, BF), "dl": sb(256, F32), "yxs": sb(512, F32), "ynbs": sb(256, F32),
 }
 for _n in ("pTa", "pTb", "pW", "pF", "pI", "pSa", "pSb", "pSc"):
     SCRATCH[_n] = ("psum", [128, 512], F32)
@@ -33,11 +35,9 @@ SEMAPHORES = ["cV", "cS", "cP", "cG", "ldxa", "ldxb", "ldn", "ldd", "ldr", "sty"
               "aw0", "aw1", "aw2", "al0", "al1", "al2"]
 
 CA = [12, 16, 16]
-VK = (1, 2)
-VKL = 2
 FPRE, FMID = 5, 2
 SLA = (128, 192)
-SLL = (112, 192, 224)
+SLL = (128, 192, 232)
 
 
 def rank_program(g, core, T, topo):
@@ -92,8 +92,13 @@ def rank_program(g, core, T, topo):
             ins = PE.matmul(o, l, rr, start and i == 0, stop and i == len(mms) - 1)
         return ins
 
-    others = [T.cores[(q + i) % NR] for i in range(1, NR)]
-    others.sort(key=lambda c: topo.die(c) == topo.die(core))
+    near = [c for c in T.cores if topo.die(c) == topo.die(core)]
+    far = [c for c in T.cores if topo.die(c) != topo.die(core)]
+    me = near.index(core)
+    others = []
+    for i in range(max(len(near), len(far))):
+        others += far[(me + i) % len(far):][:1] if i < len(far) else []
+        others += near[(me + i + 1) % len(near):][:1] if i + 1 < len(near) else []
     emask = -1
     for c in others:
         emask &= topo.mask(core, c)
@@ -118,6 +123,9 @@ def rank_program(g, core, T, topo):
     cq = T.cb[:, 16:528]
     va = 16 * CA[0]
 
+    def fill(name, n, value):
+        op("G", lambda: g.iota(T[name][:], [[0, n]], value, 0, allow_small_or_imprecise_dtypes=True), w=[name])
+
     op("Y", lambda: SY.dma_start(T.xi[:, 0:va], T.x0[:, 0:va]), w=["xia"], sem="ldxa")
     op("S", lambda: S.dma_start(T.xi[:, va:P], T.x0[:, va:P]), w=["xib"], sem="ldxb")
     op("Y", lambda: SY.dma_start(T.nbi[:], T.nb[:]), w=["nbi"], sem="ldn")
@@ -129,9 +137,6 @@ def rank_program(g, core, T, topo):
     op("V", lambda: V.memset(T.cb[:, 0:16], float(8 * q)), w=["c0"])
     op("V", lambda: V.memset(T.D0[:, 0:576:9], 512.0), r=["D0a"], w=["D0a"])
     op("V", lambda: V.memset(T.Z[:], 0.0), w=["Z"])
-    op("V", lambda: V.memset(T.k512[:], float(P)), w=["k512"])
-    op("V", lambda: V.memset(T.capb[:], float(CAP)), w=["capb"])
-    op("V", lambda: V.memset(T.k2048[:], 2048.0), w=["k2048"])
     op("G", lambda: g.affine_select(T.B1[:], T.ones[:], [[-16, 8], [0, 16]], A.is_ge, 0.0, 0, 1), r=["ones"], w=["B1"])
     op("G", lambda: g.affine_select(T.B[:], T.B1[:], [[16, 8], [0, 16]], A.is_ge, 0.0, 15, -1), r=["B1"], w=["B"])
     op("G", lambda: g.iota(T.pi[:], [[0, 8]], 0, 1), w=["pi"])
@@ -140,10 +145,8 @@ def rank_program(g, core, T, topo):
     op("G", lambda: g.affine_select(T.E[0:8, :], T.ones[0:8, :], [[-1, 8], [0, 16]], A.is_equal, 0.0, 0, 1), r=["ones"], w=["E"])
     for n in (576, 1152, 2304):
         op("S", lambda: S.activation(T.D0[:, n:2 * n], T.D0[:, 0:n], AF.Copy), r=["D0a"], w=["D0a"])
-    op("V", lambda: ts(T.pm[:, 0:1], T.pi[:, 0:1], 15, None, A.bitwise_and), r=["pi"], w=["pm0"])
-    op("V", lambda: ts(T.Z[:, 15:128:16], T.B[:, 0:128:16], 1.0 / 16, None, A.mult), r=["B", "Z"], w=["Z"])
-    op("V", lambda: V.tensor_copy(T.pf[:, 0:1], T.pm[:, 0:1]), r=["pm0"], w=["pf0"])
-    op("V", lambda: ts(T.vc[:], T.i32[:], T.pf[:, 0:1], None, A.add), r=["pf0", "i32"], w=["vc"])
+    for name, f in (("idf", -1.0), ("id8", 8.0), ("idm8", -8.0), ("idp", 1.0)):
+        op("S", lambda: S.activation(T[name][:], T.idb[:], AF.Copy, scale=f), r=["idb"], w=[name])
 
     def flags(t, ks):
         for k in ks:
@@ -154,15 +157,21 @@ def rank_program(g, core, T, topo):
     def total(h, v0, v1, nx):
         op("P", lambda: PE.matmul(T["pT" + h][:, 0:v1 - v0], T.B[:], nx(v0, v1), True, True), r=["B", "nx" + h], x=["pT" + h])
 
-    def infect(t, h, v0, v1, nx):
+    def infect(t, h, v0, v1, nx, between=(None, None, None)):
         qo = 8 * q if t < DAYS - 1 else 0
-        cap = T.capa if t < DAYS - 1 else T.capb
+        cap = "capa" if t < DAYS - 1 else "capb"
         c, cp, il = T.cb[:, 16 + v0:16 + v1], T.cb[:, 15 + v0:15 + v1], T.cb[:, 528 + v0:528 + v1]
         prev = "c0" if h == "a" else "cqa"
         op("V", lambda: ts(T.high[:, v0:v1], T["pT" + h][:, 0:v1 - v0], -TH + 0.5, None, A.is_le), w=["high" + h], x=["pT" + h])
-        op("V", lambda: V.tensor_tensor_scan(c, T.high[:, v0:v1], cap[:, v0:v1], T.cb[:, 15 + v0:16 + v0], A.add, A.min),
-           r=["high" + h, "capa", "capb", prev], w=["cq" + h])
+        if between[0]:
+            between[0]()
+        op("V", lambda: V.tensor_tensor_scan(c, T.high[:, v0:v1], T[cap][:, v0:v1], T.cb[:, 15 + v0:16 + v0], A.add, A.min),
+           r=["high" + h, cap, prev], w=["cq" + h])
+        if between[1]:
+            between[1]()
         op("V", lambda: V.tensor_tensor_scan(il, c, cp, 0.0, A.max, A.subtract), r=["cq" + h, prev], w=["ill" + h])
+        if between[2]:
+            between[2]()
         names = ["blk%d%s" % (t, h)]
         if h == "b":
             op("V", lambda: ts(win[t][:, WB * q + P:WB * (q + 1)], T.cb[:, 520:528], float(-qo), None, A.add), r=["cqb"], w=["tail%d" % t])
@@ -175,10 +184,11 @@ def rank_program(g, core, T, topo):
         qo = 8 * q if t < DAYS - 1 else 0
         op("P", lambda: group([(T.pW[:, 0:64], Wr[r], T.cb[:, 16 + r:1040:16]) for r in range(16)]),
            r=["Z", "cqa", "cqb", "illa", "illb"], x=["pW"])
-        op("V", lambda: ts(T.G[:, 8::9], nx(0, P), 8.0, 0.0, A.add, A.min), r=["nxa", "nxb"], w=["G8"])
+        op("V", lambda: ts(T.G[:, 8:2304:9], nx(0, 256), 8.0, 0.0, A.add, A.min), r=["nxa", "nxb"], w=["G8a"])
         op("V", lambda: ts(T.pa[:], T.pW[:, 32:64], 1024.0, -512.0, A.mult, A.add), w=["pa"], x=["pW"])
         op("V", lambda: ts(iw[t][:], T.pW[:, 32:64], 512.0, None, A.mult), w=["iw%d" % t], x=["pW"])
         op("V", lambda: V.tensor_tensor(T.pb[:], T.pa[:], T.vc[:], A.max), r=["pa", "vc"], w=["pb"])
+        op("V", lambda: ts(T.G[:, 2312::9], nx(256, P), 8.0, 0.0, A.add, A.min), r=["nxa", "nxb"], w=["G8"])
         op("V", lambda: V.tensor_tensor(T.pc[:], T.pb[:], T.pW[:, 0:32], A.subtract), r=["pb"], w=["pc"], x=["pW"])
         op("V", lambda: ts(T.pos[:], T.pc[:], float(qo), None, A.add), r=["pc"], w=["pos"])
         lb = ll[t][:, P * q:P * (q + 1)]
@@ -196,34 +206,37 @@ def rank_program(g, core, T, topo):
     total("a", 0, va, nx0)
     op("V", lambda: ts(T.nx0[:, va:P], T.xi[:, va:P], -1.0, None, A.mult), r=["xib"], w=["nxb"])
     total("b", va, P, nx0)
-    infect(0, "a", 0, va, nx0)
-    infect(0, "b", va, P, nx0)
-    uninfected(0, nx0)
-    op("V", lambda: V.tensor_copy(T.rb[0:8, :], T.ri[0:8, :]), r=["ri"], w=["rb"])
+    infect(0, "a", 0, va, nx0, (
+        lambda: op("V", lambda: ts(T.pm[:, 0:1], T.pi[:, 0:1], 15, None, A.bitwise_and), r=["pi"], w=["pm0"]),
+        lambda: op("V", lambda: ts(T.Z[:, 15:128:16], T.B[:, 0:128:16], 1.0 / 16, None, A.mult), r=["B", "Z"], w=["Z"]),
+        lambda: op("V", lambda: V.tensor_copy(T.pf[:, 0:1], T.pm[:, 0:1]), r=["pm0"], w=["pf0"])))
+    infect(0, "b", va, P, nx0, (
+        lambda: op("V", lambda: ts(T.vc[:], T.i32[:], T.pf[:, 0:1], None, A.add), r=["pf0", "i32"], w=["vc"]),
+        lambda: op("V", lambda: V.tensor_copy(T.idh[:], T.idb[:]), r=["idb"], w=["idh"]), None))
+    fill("k512", 8, P)
     op("V", lambda: ts(T.t1[:], T.nbi[:], 3584, None, A.bitwise_and), r=["nbi"], w=["t1"])
+    uninfected(0, nx0)
+    fill("capb", P, CAP)
+    fill("kneg", 128, -8 * UB)
+    fill("kpos", 128, 2048 + 8 * UB)
+    op("V", lambda: V.tensor_copy(T.rb[0:8, :], T.ri[0:8, :]), r=["ri"], w=["rb"])
+    op("V", lambda: ts(T.t2[:], T.t1[:], 1.0 / 64, -2048.0, A.mult, A.add), r=["t1"], w=["t2"])
     op("P", lambda: PE.matmul(T.pTa[:], T.E[0:8, :], T.rb[0:8, :], True, True), r=["E", "rb"], x=["pTa"])
     op("S", lambda: S.activation(T.D0[:, 8::9], T.pTa[:], AF.Copy), r=["D0a"], w=["D0a"], x=["pTa"])
     op("V", lambda: ts(T.t3[:], T.d0[:], float(STEP), None, A.add), r=["d0"], w=["t3"])
-    op("V", lambda: ts(T.t2[:], T.t1[:], 1.0 / 64, -2048.0, A.mult, A.add), r=["t1"], w=["t2"])
-    op("V", lambda: ts(T.d1[:], T.t3[:], 2047, None, A.bitwise_and), r=["t3"], w=["d1"])
     op("V", lambda: V.tensor_tensor(T.L[:], T.t2[:], T.nbi[:], A.add), r=["t2", "nbi"], w=LN)
-    op("V", lambda: V.tensor_copy(T.idh[:], T.idb[:]), r=["idb"], w=["idh"])
-    op("V", lambda: ts(T.off[:], T.L[:], 2048.0, None, A.add), r=LN, w=["off"])
-    op("V", lambda: ts(T.idf[:], T.idb[:], -1.0, None, A.mult), r=["idb"], w=["idf"])
-    op("V", lambda: ts(T.t3[:], T.d0[:], float(2 * STEP), None, A.add), r=["d0"], w=["t3"])
-    op("V", lambda: ts(T.d2[:], T.t3[:], 2047, None, A.bitwise_and), r=["t3"], w=["d2"])
-
-    def index_terms(out, a, b):
-        return [(out, T.idh[:], T.jh[:, a:b])] + [(out, T.idb[:], T.tm[:, 256 * i + a:256 * i + b]) for i in range(7)]
+    op("V", lambda: ts(T.d1[:], T.t3[:], 2047, None, A.bitwise_and), r=["t3"], w=["d1"])
+    op("V", lambda: ts(T.off[:], T.L[:], 2048.0, None, A.add), r=LN, w=["off", "off0"])
+    op("V", lambda: ts(T.t4[:], T.d0[:], float(2 * STEP), None, A.add), r=["d0"], w=["t4"])
 
     for t in range(DAYS):
         last = t == DAYS - 1
         wn = ["win%d" % t, "blk%da" % t, "blk%db" % t, "tail%d" % t]
         w = win[t][:]
-        ln = ["ll%d" % t, "lb%d" % t, "idx"]
         tmn = ["jh", "idh", "idb"] + ["tm%d" % i for i in range(7)]
         bounds = (0,) + SLA + (256,) if not last else (0, SLL[0], SLL[1], 256)
         banks = ["pSa", "pSb", "pSc"]
+        pieces = [(banks[i], bounds[i], bounds[i + 1], T[banks[i]][:, 0:bounds[i + 1] - bounds[i]]) for i in range(3)]
 
         def pick(e, out, src, r, names):
             if e == "V":
@@ -232,20 +245,24 @@ def rank_program(g, core, T, topo):
                 op("S", lambda: S.activation(out, src, AF.Copy), r=r, w=names)
 
         def gather(e, k, c0, c1, names):
-            pick(e, T.G[:, 144 * c0 + k:144 * c1:9], w.indirect(T.off[:, 32 * k + c0:32 * k + c1]), wn + ["off"], names)
+            pick(e, T.G[:, 144 * c0 + k:144 * c1:9], w.indirect(T.off[:, 32 * k + c0:32 * k + c1]),
+                 wn + (["off0"] if 32 * k + c1 <= SLA[1] else ["off", "off0"]), names)
 
         def slg(e, c0, c1, name):
-            pick(e, T.SG[:, 16 * c0:16 * c1], ll[t][:].indirect(T.idx[:, c0:c1]), ln, [name])
+            pick(e, T.SG[:, 16 * c0:16 * c1], ll[t][:].indirect(T.idx[:, c0:c1]), ["ll%d" % t, "lb%d" % t, "idx"], [name])
 
         def counts():
             op("V", lambda: V.tensor_tensor_scan(T.C[:], T.k512[:], win[t][:, WB - 1::WB], 0.0, A.add, A.subtract), r=wn + ["k512"], w=["C"])
             op("V", lambda: V.tensor_copy(T.nf[:], win[t][:, WB - 1::WB]), r=wn, w=["nf"])
-
-        def scale():
             op("V", lambda: ts(T.cs[:, 0:1], T.C[:, 7:8], 1.0 / 2048, None, A.mult), r=["C"], w=["cs"])
 
-        def places():
+        def place():
             op("V", lambda: ts(T.ju[:], dd[t][:], T.cs[:, 0:1], -0.5 + 2.0 ** -12, A.mult, A.add), r=["cs", "d%d" % t], w=["ju"])
+
+        def index_terms(out, c0, c1):
+            return [(out, T.idh[:], T.jh[:, c0:c1])] + [(out, T.idb[:], T.tm[:, 256 * i + c0:256 * i + c1]) for i in range(7)]
+
+        def terms():
             op("V", lambda: ts(T.jh[:], T.ju[:], -2048.0, None, A.add), r=["ju"], w=["jh"])
             for i in range(7):
                 op("V", lambda: ts(T.tm[:, 256 * i:256 * (i + 1)], T.ju[:], T.C[:, i:i + 1], T.nf[:, i:i + 1], A.is_ge, A.mult),
@@ -257,31 +274,36 @@ def rank_program(g, core, T, topo):
 
         def update(v0, v1, hs):
             op("V", lambda: V.tensor_tensor_scan(T.O[:, 9 * v0:9 * v1], T.D0[:, 9 * v0:9 * v1], T.G[:, 9 * v0:9 * v1], 0.0, A.add, A.min),
-               r=["G%s%d" % (h, k) for k in range(8) for h in hs] + ["G8", "D0a"], w=["nx" + h for h in hs])
+               r=["G%s%d" % (h, k) for k in range(8) for h in hs] + ["G8", "G8a", "D0a"], w=["nx" + h for h in hs])
 
         def prewrap():
-            for i in range(3):
-                c0, c1 = bounds[i], bounds[i + 1]
-                out = T[banks[i]][:, 0:c1 - c0]
+            for bank, c0, c1, out in pieces:
                 mm = index_terms(out, c0, c1) + [(out, T.idf[:], T.L[:, c0:c1])]
                 if last:
-                    mm.append((out, T.idb[:], T.k2048[:, 0:c1 - c0]))
-                op("P", lambda: group(mm, stop=False), r=tmn + LN + ["idf", "k2048"], x=[banks[i]])
+                    mm += [(out, T.idb[:], T.kneg[:, 0:c1 - c0]), (out, T.id8[:], T.ub[:, c0:c1])]
+                op("P", lambda: group(mm, stop=False), r=tmn + LN + ["idf", "kneg", "id8", "ub"], x=[bank])
+
+        def plain():
+            for c0 in (0, 128):
+                out = T.pW[:, 256 + c0:384 + c0]
+                op("P", lambda: group([(out, T.idp[:], T.L[:, c0:c0 + 128]), (out, T.idm8[:], T.ub[:, c0:c0 + 128]), (out, T.idb[:], T.kpos[:])]),
+                   r=LN + ["idp", "idm8", "ub", "kpos"], x=["pW"])
 
         def wrap(i, names):
-            c0, c1 = bounds[i], bounds[i + 1]
-            out = T[banks[i]][:, 0:c1 - c0]
-            op("P", lambda: group([(out, Wr[r], T.SG[:, 16 * c0 + r:16 * c1:16]) for r in range(16)], start=False), r=["Z"] + names, x=[banks[i]])
+            bank, c0, c1, out = pieces[i]
+            op("P", lambda: group([(out, Wr[r], T.SG[:, 16 * c0 + r:16 * c1:16]) for r in range(16)], start=False), r=["Z"] + names, x=[bank])
 
-        def select(i):
-            c0, c1 = bounds[i], bounds[i + 1]
-            dl = T.pW[:, 256 + c0:256 + c1]
-            op("V", lambda: V.tensor_tensor(dl, T[banks[i]][:, 0:c1 - c0], T.h[:, c0:c1], A.mult), r=["h"], w=["dl%d" % i], x=[banks[i], "pW"])
-            if last:
-                op("V", lambda: V.tensor_tensor(T.ynbs[:, c0:c1], dl, T.L[:, c0:c1], A.add), r=["dl%d" % i, LN[i]], w=["yn%d" % i], x=["pW"])
+        def select(i, step):
+            bank, c0, c1, out = pieces[i]
+            pw = T.pW[:, 256 + c0:256 + c1]
+            if step == 0:
+                op("V", lambda: V.tensor_tensor(T.dl[:, c0:c1] if last else pw, out, T.h[:, c0:c1], A.mult), r=["h"], w=["dl%d" % i],
+                   x=[bank] + ([] if last else ["pW"]))
+            elif last:
+                op("V", lambda: V.tensor_tensor(T.ynbs[:, c0:c1], pw, T.dl[:, c0:c1], A.add), r=["dl%d" % i], w=["yn%d" % i], x=["pW"])
                 op("Y", lambda: SY.dma_start(T.ynb[:, c0:c1], T.ynbs[:, c0:c1]), r=["yn%d" % i], sem="stn%d" % i)
             else:
-                op("V", lambda: V.tensor_tensor(T.L[:, c0:c1], dl, T.L[:, c0:c1], A.add), r=["dl%d" % i], w=[LN[i]], x=["pW"])
+                op("V", lambda: V.tensor_tensor(T.L[:, c0:c1], pw, T.L[:, c0:c1], A.add), r=["dl%d" % i], w=[LN[i]], x=["pW"])
 
         def hit():
             op("V", lambda: ts(T.h[:], T.pF[:, 0:256], -30.0, None, A.is_lt), w=["h"], x=["pF"])
@@ -289,21 +311,17 @@ def rank_program(g, core, T, topo):
         if not last:
             ca = CA[t + 1]
             va = 16 * ca
-            ka, kb = 8 - VK[0], 8 - VK[1]
-            for k in range(ka):
+            for k in range(7):
                 gather("S", k, 0, ca, ["Ga%d" % k])
-            for k in range(kb):
+            for k in range(6):
                 gather("S", k, ca, 32, ["Gb%d" % k])
             counts()
-            both = list(range(ka, 8))
-            for k in both:
-                gather("V", k, 0, 32, ["Ga%d" % k, "Gb%d" % k])
-            scale()
-            for k in range(kb, ka):
-                gather("V", k, ca, 32, ["Gb%d" % k])
-            flags(t, both)
-            rest = list(range(kb, ka)) + list(range(kb))
-            places()
+            gather("V", 7, 0, 32, ["Ga7", "Gb7"])
+            place()
+            gather("V", 6, ca, 32, ["Gb6"])
+            flags(t, [7])
+            rest = [6, 0, 1, 2, 3, 4, 5]
+            terms()
             update(0, va, "a")
             total("a", 0, va, nxo)
             offsets()
@@ -311,10 +329,12 @@ def rank_program(g, core, T, topo):
                 op("V", lambda: V.memset(T.cb[:, 0:16], 0.0), w=["c0"])
             infect(t + 1, "a", 0, va, nxo)
             update(va, P, "b")
-            for i in range(3):
-                slg("S", bounds[i], bounds[i + 1], "SG%d" % i)
             flags(t, rest[:FPRE])
             total("b", va, P, nxo)
+            if t == 0:
+                op("V", lambda: ts(T.d2[:], T.t4[:], 2047, None, A.bitwise_and), r=["t4"], w=["d2"])
+            for i in range(3):
+                slg("S", bounds[i], bounds[i + 1], "SG%d" % i)
             flags(t, rest[FPRE:FPRE + FMID])
             infect(t + 1, "b", va, P, nxo)
             uninfected(t + 1, nxo)
@@ -323,27 +343,26 @@ def rank_program(g, core, T, topo):
             for i in range(3):
                 wrap(i, ["SG%d" % i])
             hit()
-            for i in range(3):
-                select(i)
-            op("V", lambda: ts(T.off[:], T.L[:], 2048.0, None, A.add), r=LN, w=["off"])
+            for i, step in ((0, 0), (1, 0), (0, 1), (1, 1)):
+                select(i, step)
+            op("V", lambda: ts(T.off[:, 0:SLA[1]], T.L[:, 0:SLA[1]], 2048.0, None, A.add), r=LN[:2], w=["off0"])
+            select(2, 0)
+            select(2, 1)
+            op("V", lambda: ts(T.off[:, SLA[1]:], T.L[:, SLA[1]:], 2048.0, None, A.add), r=LN[2:], w=["off"])
         else:
-            ks = 8 - VKL
-            for k in range(ks):
+            for k in range(6):
                 gather("S", k, 0, 32, ["Ga%d" % k, "Gb%d" % k])
             counts()
-            op("V", lambda: ts(T.t1[:], T.L[:], 1.0 / WB, 2048.0 / WB - 0.499, A.mult, A.add), r=LN, w=["t1"])
-            scale()
-            op("V", lambda: ts(T.t2[:], T.t1[:], -8.0, 2048.0, A.mult, A.add), r=["t1"], w=["t2"])
+            op("V", lambda: ts(T.ub[:], T.L[:], 1.0 / WB, UB + 2048.0 / WB - 0.492, A.mult, A.add), r=LN, w=["ub"])
+            place()
+            plain()
             flags(t, [0, 1])
-            places()
-            op("V", lambda: V.tensor_tensor(T.L[:], T.L[:], T.t2[:], A.add), r=["t2"], w=LN)
+            terms()
             gather("V", 7, 0, 32, ["Ga7", "Gb7"])
             offsets()
-            for k in range(ks, 7):
-                gather("V", k, 0, 32, ["Ga%d" % k, "Gb%d" % k])
-            flags(t, [2, 3])
+            gather("V", 6, 0, 32, ["Ga6", "Gb6"])
+            flags(t, [2, 7, 3, 4, 6, 5])
             prewrap()
-            flags(t, [7, 4, 6, 5])
             a, b, c = SLL
             slg("S", 0, a, "SG0")
             update(0, P, "ab")
@@ -351,13 +370,13 @@ def rank_program(g, core, T, topo):
             op("S", lambda: S.activation(T.yxs[:], T.O[:, 8::9], AF.Copy, scale=-1.0), r=["nxa", "nxb"], w=["yxs"])
             op("Y", lambda: SY.dma_start(T.yx[:], T.yxs[:]), r=["yxs"], sem="sty")
             slg("S", b, c, "SG2")
+            hit()
             slg("V", c, 256, "SG3")
             wrap(0, ["SG0"])
             wrap(1, ["SG1"])
             wrap(2, ["SG2", "SG3"])
-            hit()
-            for i in range(3):
-                select(i)
+            for i, step in ((0, 0), (1, 0), (0, 1), (1, 1), (2, 0), (2, 1)):
+                select(i, step)
 
     g.wait_ge(T.sem.sent, sent["sent"])
     for s in ("cV", "cS", "cP", "cG"):

@@ -20,24 +20,29 @@ SCRATCH = {
     "ones": sb(128, BF), "B1": sb(128, BF), "B": sb(128, BF), "idb": sb(128, BF), "idh": sb(128, F16), "idf": sb(128, F32),
     "id8": sb(128, BF), "idm8": sb(128, BF), "idp": sb(128, F32),
     "E": sb(128, BF), "Z": sb(144, BF), "kneg": sb(128, BF), "kpos": sb(128, BF),
-    "high": sb(512, BF), "cb": sb(1040, BF), "capa": sb(512, BF), "capb": sb(512, BF),
+    "high": sb(512, BF), "cb": sb(1040, BF), "cap": sb(512, BF), "kq": sb(512, BF),
     "pi": sb(8, I32), "pm": sb(8, I32), "pf": sb(8, F32), "i32": sb(32, I32), "vc": sb(32, F32),
-    "pa": sb(32, F32), "pb": sb(32, F32), "pc": sb(32, F32), "pos": sb(32, U16),
-    "iw0": sb(32, BF), "iw1": sb(32, BF), "iw2": sb(32, BF),
+    "pa0": sb(32, BF), "pa1": sb(32, BF), "pa2": sb(32, BF), "pb": sb(32, F32), "pc": sb(32, F32), "pos": sb(32, U16),
     "k512": sb(8, F32), "C": sb(8, F32), "cs": sb(8, F32), "nf": sb(8, F32),
     "t1": sb(256, I32), "t2": sb(256, F32), "t3": sb(256, I32), "t4": sb(256, I32), "d1": sb(256, I32), "d2": sb(256, I32),
-    "L": sb(256, F32), "off": sb(256, U16), "ju": sb(256, U16), "jh": sb(256, F16), "tm": sb(7 * 256, BF),
-    "idx": sb(256, U16), "h": sb(256, F32), "ub": sb(256, BF), "dl": sb(256, F32), "yxs": sb(512, F32), "ynbs": sb(256, F32),
+    "L": sb(256, F32), "off": sb(256, U16), "ju": sb(256, U16), "jh": sb(256, F16), "ih": sb(256, F16), "tm": sb(7 * 256, BF),
+    "idx": sb(256, U16), "h": sb(256, F32), "ub": sb(256, BF), "Lf": sb(256, F32), "yxs": sb(512, F32), "ynbs": sb(256, F32),
 }
 for _n in ("pTa", "pTb", "pW", "pF", "pI", "pSa", "pSb", "pSc"):
     SCRATCH[_n] = ("psum", [128, 512], F32)
 SEMAPHORES = ["cV", "cS", "cP", "cG", "ldxa", "ldxb", "ldn", "ldd", "ldr", "sty", "stn0", "stn1", "stn2", "sent",
               "aw0", "aw1", "aw2", "al0", "al1", "al2"]
 
-CA = [12, 16, 16]
-FPRE, FMID = 5, 2
-SLA = (128, 192)
-SLL = (128, 192, 232)
+CA = [8, 16, 16]
+SLA = (0, 128, 192, 256)
+
+START = """nxa ta ia0 ia1 g8a ia2 ia3 Z t1 nxb t2 t4 tb pm ib0 rb ib1 pf ib4 ib2 vc ib3 pw idh d2 L res pa g8b pb t3 off kneg pc
+kpos k512 d1 pos scat"""
+DAY = """C a5S a1V cs nf a4S a6V ju b6V a2V a7S t5 b7S t4 t2 t6 t0 jh a0S t3 f7 a3S b3S f6 t1 p0 ua x0 p1 b2S p2 b1V b5S ta f2 f1
+b4S b0S ia0 f4 x1 x2 ia1 ub ia2 f3 ih tb s2S ia3 ib0 f5 g8b ib1 f0 ib2 ib4 s3V s5S pw pa l1 s4S w1 ib3 s0S l2 s1S pb h0 l0 h1
+s7S pc g8a w0 m1 s6S w2 pos h2 n1 scat m0 o1 m2 n0 n2 o0 o2"""
+LAST = """C blk plain c0S cs nf ju t2 t6 t5 f0 c1S t0 c3S t1 t4 f1 jh t3 c5V c7V p1 p0 x0 p2 f5 c2S c4S x1 c6V x2 f7 s4V f2 ih u
+f6 l0 l2 f3 f4 s5V s2S s7V l1 s1S h0 h1 s0S h2 s3S w0 yx m0 w1 s6S m1 n0 n1 w2 m2 n2"""
 
 
 def rank_program(g, core, T, topo):
@@ -46,7 +51,7 @@ def rank_program(g, core, T, topo):
         return
     V, S, PE, SY = g.vector, g.scalar, g.tensor, g.sync
     Q = {"V": V, "S": S, "P": PE, "G": g, "Y": SY}
-    count = {"cV": 0, "cS": 0, "cP": 0, "cG": 0}
+    count = {}
     known = {k: {} for k in Q}
     writer, readers = {}, {}
 
@@ -66,19 +71,15 @@ def rank_program(g, core, T, topo):
         for ev in sorted(evs, key=lambda z: -z[1]):
             need(e, ev)
         ins = fn()
-        if sem is None:
-            sem = "c" + e
-            count[sem] += 1
-            ins.then_inc(T.sem[sem], 1)
-            ev = (sem, count[sem], dict(known[e]))
-        else:
-            ins.then_inc(T.sem[sem], 16)
-            ev = (sem, 16, dict(known[e]))
-            e = "dma"
+        inc = 1 if sem is None else 16
+        sem, who = ("c" + e, e) if sem is None else (sem, "dma")
+        count[sem] = count.get(sem, 0) + inc
+        ins.then_inc(T.sem[sem], inc)
+        ev = (sem, count[sem], dict(known[e]))
         for k in r:
-            readers.setdefault(k, []).append((e, ev))
+            readers.setdefault(k, []).append((who, ev))
         for k in tuple(w) + tuple(x):
-            writer[k] = (e, ev)
+            writer[k] = (who, ev)
             readers[k] = []
 
     def ts(out, in0, s1, s2, o0, o1=None):
@@ -118,14 +119,147 @@ def rank_program(g, core, T, topo):
     win = [T.win0, T.win1, T.win2]
     ll = [T.ll0, T.ll1, T.ll2]
     dd = [T.d0, T.d1, T.d2]
-    iw = [T.iw0, T.iw1, T.iw2]
+    pa = [T.pa0, T.pa1, T.pa2]
     Wr = [T.Z[:, 15 - r:143 - r] for r in range(16)]
     cq = T.cb[:, 16:528]
-    va = 16 * CA[0]
+    LN = ["L0", "L1", "L2"]
+    banks = ["pSa", "pSb", "pSc"]
+    pieces = [(banks[i], SLA[i], SLA[i + 1], T[banks[i]][:, 0:SLA[i + 1] - SLA[i]]) for i in range(3)]
+
+    def vop(fn, **kw):
+        return lambda: op("V", fn, **kw)
+
+    def pop(fn, **kw):
+        return lambda: op("P", fn, **kw)
 
     def fill(name, n, value):
-        op("G", lambda: g.iota(T[name][:], [[0, n]], value, 0, allow_small_or_imprecise_dtypes=True), w=[name])
+        return lambda: op("G", lambda: g.iota(T[name][:], [[0, n]], value, 0, allow_small_or_imprecise_dtypes=True), w=[name])
 
+    def sending(t, nx):
+        va, step = 16 * CA[t], {}
+        for h, v0, v1 in (("a", 0, va), ("b", va, P)):
+            def part(h=h, v0=v0, v1=v1):
+                c, cp, il = T.cb[:, 16 + v0:16 + v1], T.cb[:, 15 + v0:15 + v1], T.cb[:, 528 + v0:528 + v1]
+                prev, bank, blk = "c0" if h == "a" else "cqa", "pT" + h, "blk%d%s" % (t, h)
+                step["t" + h] = pop(lambda: PE.matmul(T[bank][:, 0:v1 - v0], T.B[:], nx(v0, v1), True, True), r=["B", "nx" + h], x=[bank])
+                step["i%s0" % h] = vop(lambda: ts(T.high[:, v0:v1], T[bank][:, 0:v1 - v0], -TH + 0.5, None, A.is_le), w=["high" + h], x=[bank])
+                step["i%s1" % h] = vop(lambda: V.tensor_tensor_scan(c, T.high[:, v0:v1], T.cap[:, v0:v1], T.cb[:, 15 + v0:16 + v0], A.add, A.min),
+                                       r=["high" + h, "cap", prev], w=["cq" + h])
+                step["i%s2" % h] = vop(lambda: V.tensor_tensor_scan(il, c, cp, 0.0, A.max, A.subtract), r=["cq" + h, prev], w=["ill" + h])
+
+                def send():
+                    op("V", lambda: V.tensor_tensor_scan(win[t][:, WB * q + v0:WB * q + v1], il, nx(v0, v1), 0.0, A.max, A.mult),
+                       r=["ill" + h, "nx" + h] + ([] if h == "a" else ["tail%d" % t]), w=[blk])
+                    allgather(win[t][:, WB * q + v0:WB * q + (v1 if h == "a" else WB)], [blk], "aw%d" % t, "win%d" % t)
+                step["i%s3" % h] = send
+            part()
+        step["ib4"] = vop(lambda: V.tensor_copy(win[t][:, WB * q + P:WB * (q + 1)], T.cb[:, 520:528]), r=["cqb"], w=["tail%d" % t])
+        step["pw"] = pop(lambda: group([(T.pW[:, 0:64], Wr[r], T.cb[:, 16 + r:1040:16]) for r in range(16)]),
+                         r=["Z", "cqa", "cqb", "illa", "illb"], x=["pW"])
+        step["g8a"] = vop(lambda: ts(T.G[:, 8:9 * va:9], nx(0, va), 8.0, 0.0, A.add, A.min), r=["nxa"], w=["G8a"])
+        step["g8b"] = vop(lambda: ts(T.G[:, 9 * va + 8::9], nx(va, P), 8.0, 0.0, A.add, A.min), r=["nxb"], w=["G8b"])
+        step["pa"] = vop(lambda: ts(pa[t][:], T.pW[:, 32:64], 1024.0, -512.0, A.mult, A.add), w=["pa%d" % t], x=["pW"])
+        step["pb"] = vop(lambda: V.tensor_tensor(T.pb[:], pa[t][:], T.vc[:], A.max), r=["pa%d" % t, "vc"], w=["pb"])
+        step["pc"] = vop(lambda: V.tensor_tensor(T.pc[:], T.pb[:], T.pW[:, 0:32], A.subtract), r=["pb"], w=["pc"], x=["pW"])
+        step["pos"] = vop(lambda: V.tensor_copy(T.pos[:], T.pc[:]), r=["pc"], w=["pos"])
+
+        def scatter():
+            lb = ll[t][:, P * q:P * (q + 1)]
+            if t < DAYS - 1:
+                op("V", lambda: V.tensor_tensor(lb.indirect(T.pos[:]), cq, T.kq[:], A.add), r=["pos", "cqa", "cqb", "kq"], w=["lb%d" % t])
+            else:
+                op("V", lambda: V.tensor_copy(lb.indirect(T.pos[:]), cq), r=["pos", "cqa", "cqb"], w=["lb%d" % t])
+            allgather(lb, ["lb%d" % t], "al%d" % t, "ll%d" % t)
+        step["scat"] = scatter
+        return step
+
+    def nx0(v0, v1):
+        return T.nx0[:, v0:v1]
+
+    def nxo(v0, v1):
+        return T.O[:, 9 * v0 + 8:9 * v1:9]
+
+    def daily(t):
+        last, step = t == DAYS - 1, {}
+        ca = CA[min(t + 1, DAYS - 1)]
+        wn = ["win%d" % t, "blk%da" % t, "blk%db" % t]
+        nf = win[t][:, WB - 1::WB]
+
+        def pick(e, out, src, r, names):
+            if e == "V":
+                return vop(lambda: V.tensor_copy(out, src), r=r, w=names)
+            return lambda: op("S", lambda: S.activation(out, src, AF.Copy), r=r, w=names)
+
+        for k in range(8):
+            i = max(i for i in range(3) if SLA[i] <= 32 * k)
+            for e in "VS":
+                for h, c0, c1, hs in (("a", 0, ca, "a"), ("b", ca, 32, "b"), ("c", 0, 32, "ab")):
+                    step["%s%d%s" % (h, k, e)] = pick(e, T.G[:, 144 * c0 + k:144 * c1:9], win[t][:].indirect(T.off[:, 32 * k + c0:32 * k + c1]),
+                                                      wn + ["off%d" % i], ["G%s%d" % (x, k) for x in hs])
+                step["s%d%s" % (k, e)] = pick(e, T.SG[:, 512 * k:512 * k + 512], ll[t][:].indirect(T.idx[:, 32 * k:32 * k + 32]),
+                                              ["ll%d" % t, "lb%d" % t, "idx%d" % i], ["SG%d" % k])
+
+            def flags(k=k):
+                out = T.pF[:, 32 * k:32 * k + 32]
+                mm = [(out, Wr[r], T.G[:, 9 * r + k::144]) for r in range(16)] + [(out, T.idb[:], pa[t][:])]
+                op("P", lambda: group(mm), r=["Z", "idb", "pa%d" % t, "Ga%d" % k, "Gb%d" % k], w=["F%d" % k], x=["pF"])
+            step["f%d" % k] = flags
+        for name, v0, v1, hs in (("ua", 0, 16 * ca, "a"), ("ub", 16 * ca, P, "b"), ("u", 0, P, "ab")):
+            step[name] = vop(lambda v0=v0, v1=v1: V.tensor_tensor_scan(T.O[:, 9 * v0:9 * v1], T.D0[:, 9 * v0:9 * v1], T.G[:, 9 * v0:9 * v1], 0.0, A.add, A.min),
+                             r=["G%s%d" % (h, k) for k in range(8) for h in hs] + ["G8a", "G8b", "D0a"], w=["nx" + h for h in hs])
+        step["C"] = vop(lambda: V.tensor_tensor_scan(T.C[:], T.k512[:], nf, 0.0, A.add, A.subtract), r=wn + ["k512"], w=["C"])
+        step["cs"] = vop(lambda: ts(T.cs[:, 0:1], T.C[:, 7:8], 1.0 / 2048, None, A.mult), r=["C"], w=["cs"])
+        step["ju"] = vop(lambda: ts(T.ju[:], dd[t][:], T.cs[:, 0:1], -0.5 + 2.0 ** -12, A.mult, A.add), r=["cs", "d%d" % t], w=["ju"])
+        step["jh"] = vop(lambda: ts(T.jh[:], T.ju[:], -2048.0, None, A.add), r=["ju"], w=["jh"])
+        step["ih"] = vop(lambda: ts(T.ih[:], T.idx[:], -2048.0, None, A.add), r=["idx0", "idx1", "idx2"], w=["ih"])
+        for i in range(7):
+            step["t%d" % i] = vop(lambda i=i: ts(T.tm[:, 256 * i:256 * (i + 1)], T.ju[:], T.C[:, i:i + 1], T.nf[:, i:i + 1], A.is_ge, A.mult),
+                                  r=["ju", "C", "nf"], w=["tm%d" % i])
+        step["nf"] = vop(lambda: V.tensor_copy(T.nf[:], nf), r=wn, w=["nf"])
+        for i, (bank, c0, c1, out) in enumerate(pieces):
+            def piece(i=i, bank=bank, c0=c0, c1=c1, out=out):
+                ks = range(c0 // 32, c1 // 32)
+                mm = [(out, T.idh[:], T.jh[:, c0:c1])] + [(out, T.idb[:], T.tm[:, 256 * j + c0:256 * j + c1]) for j in range(7)]
+                step["p%d" % i] = pop(lambda: group(mm), r=["jh", "idh", "idb"] + ["tm%d" % j for j in range(7)], x=[bank])
+                step["x%d" % i] = vop(lambda: ts(T.idx[:, c0:c1], out, 2048.0, None, A.add), w=["idx%d" % i], x=[bank])
+                ml = [(out, T.idh[:], T.ih[:, c0:c1]), (out, T.idf[:], T.L[:, c0:c1])]
+                if last:
+                    ml += [(out, T.idb[:], T.kneg[:, 0:c1 - c0]), (out, T.id8[:], T.ub[:, c0:c1])]
+                step["l%d" % i] = pop(lambda: group(ml, stop=False), r=[LN[i], "ih", "idf", "kneg", "id8", "ub"], x=[bank])
+                step["w%d" % i] = pop(lambda: group([(out, Wr[r], T.SG[:, 16 * c0 + r:16 * c1:16]) for r in range(16)], start=False),
+                                      r=["Z"] + ["SG%d" % k for k in ks], x=[bank])
+                step["h%d" % i] = vop(lambda: ts(T.h[:, c0:c1], T.pF[:, c0:c1], -542.0, None, A.is_lt), r=["F%d" % k for k in ks], w=["h%d" % i], x=["pF"])
+                pw = T.pI[:, 256 + c0:256 + c1]
+                if last:
+                    step["m%d" % i] = vop(lambda: V.tensor_tensor(T.Lf[:, c0:c1], out, T.h[:, c0:c1], A.mult), r=["h%d" % i], w=["dl%d" % i], x=[bank])
+
+                    def store():
+                        op("V", lambda: V.tensor_tensor(T.ynbs[:, c0:c1], T.pI[:, c0:c1], T.Lf[:, c0:c1], A.add), r=["dl%d" % i], w=["yn%d" % i], x=["pI"])
+                        op("Y", lambda: SY.dma_start(T.ynb[:, c0:c1], T.ynbs[:, c0:c1]), r=["yn%d" % i], sem="stn%d" % i)
+                    step["n%d" % i] = store
+                else:
+                    step["m%d" % i] = vop(lambda: V.tensor_tensor(pw, out, T.h[:, c0:c1], A.mult), r=["h%d" % i], w=["dl%d" % i], x=[bank, "pI"])
+                    step["n%d" % i] = vop(lambda: V.tensor_tensor(T.L[:, c0:c1], pw, T.L[:, c0:c1], A.add), r=["dl%d" % i], w=[LN[i]], x=["pI"])
+                    step["o%d" % i] = vop(lambda: ts(T.off[:, c0:c1], T.L[:, c0:c1], 2048.0, None, A.add), r=[LN[i]], w=["off%d" % i])
+            piece()
+        step["blk"] = vop(lambda: ts(T.ub[:], T.L[:], 1.0 / WB, UB + 2048.0 / WB - 0.492, A.mult, A.add), r=LN, w=["ub"])
+
+        def plain():
+            for c0 in (0, 128):
+                out = T.pI[:, c0:128 + c0]
+                op("P", lambda: group([(out, T.idp[:], T.L[:, c0:c0 + 128]), (out, T.idm8[:], T.ub[:, c0:c0 + 128]), (out, T.idb[:], T.kpos[:])]),
+                   r=LN + ["idp", "idm8", "ub", "kpos"], x=["pI"])
+        step["plain"] = plain
+
+        def loads():
+            op("S", lambda: S.activation(T.yxs[:], T.O[:, 8::9], AF.Copy, scale=-1.0), r=["nxa", "nxb"], w=["yxs"])
+            op("Y", lambda: SY.dma_start(T.yx[:], T.yxs[:]), r=["yxs"], sem="sty")
+        step["yx"] = loads
+        if not last:
+            step.update(sending(t + 1, nxo))
+        return step
+
+    va = 16 * CA[0]
     op("Y", lambda: SY.dma_start(T.xi[:, 0:va], T.x0[:, 0:va]), w=["xia"], sem="ldxa")
     op("S", lambda: S.dma_start(T.xi[:, va:P], T.x0[:, va:P]), w=["xib"], sem="ldxb")
     op("Y", lambda: SY.dma_start(T.nbi[:], T.nb[:]), w=["nbi"], sem="ldn")
@@ -133,10 +267,11 @@ def rank_program(g, core, T, topo):
     op("Y", lambda: SY.dma_start(T.d0[:], T.dice[:]), w=["d0"], sem="ldd")
     op("V", lambda: V.memset(T.ones[:], 1.0), w=["ones"])
     op("V", lambda: V.memset(T.D0[:, 0:576], 0.0), w=["D0a"])
-    op("V", lambda: V.memset(T.capa[:], float(CAP + 8 * q)), w=["capa"])
-    op("V", lambda: V.memset(T.cb[:, 0:16], float(8 * q)), w=["c0"])
+    op("V", lambda: V.memset(T.cap[:], float(CAP)), w=["cap"])
+    op("V", lambda: V.memset(T.cb[:, 0:16], 0.0), w=["c0"])
     op("V", lambda: V.memset(T.D0[:, 0:576:9], 512.0), r=["D0a"], w=["D0a"])
     op("V", lambda: V.memset(T.Z[:], 0.0), w=["Z"])
+    op("V", lambda: V.memset(T.kq[:], float((WB - P) * q)), w=["kq"])
     op("G", lambda: g.affine_select(T.B1[:], T.ones[:], [[-16, 8], [0, 16]], A.is_ge, 0.0, 0, 1), r=["ones"], w=["B1"])
     op("G", lambda: g.affine_select(T.B[:], T.B1[:], [[16, 8], [0, 16]], A.is_ge, 0.0, 15, -1), r=["B1"], w=["B"])
     op("G", lambda: g.iota(T.pi[:], [[0, 8]], 0, 1), w=["pi"])
@@ -148,238 +283,35 @@ def rank_program(g, core, T, topo):
     for name, f in (("idf", -1.0), ("id8", 8.0), ("idm8", -8.0), ("idp", 1.0)):
         op("S", lambda: S.activation(T[name][:], T.idb[:], AF.Copy, scale=f), r=["idb"], w=[name])
 
-    def flags(t, ks):
-        for k in ks:
-            out = T.pF[:, 32 * k:32 * k + 32]
-            mm = [(out, Wr[r], T.G[:, 9 * r + k::144]) for r in range(16)] + [(out, T.idb[:], iw[t][:])]
-            op("P", lambda: group(mm), r=["Z", "idb", "iw%d" % t, "Ga%d" % k, "Gb%d" % k], x=["pF"])
+    def resist():
+        op("P", lambda: PE.matmul(T.pTa[:], T.E[0:8, :], T.rb[0:8, :], True, True), r=["E", "rb"], x=["pTa"])
+        op("S", lambda: S.activation(T.D0[:, 8::9], T.pTa[:], AF.Copy), r=["D0a"], w=["D0a"], x=["pTa"])
 
-    def total(h, v0, v1, nx):
-        op("P", lambda: PE.matmul(T["pT" + h][:, 0:v1 - v0], T.B[:], nx(v0, v1), True, True), r=["B", "nx" + h], x=["pT" + h])
-
-    def infect(t, h, v0, v1, nx, between=(None, None, None)):
-        qo = 8 * q if t < DAYS - 1 else 0
-        cap = "capa" if t < DAYS - 1 else "capb"
-        c, cp, il = T.cb[:, 16 + v0:16 + v1], T.cb[:, 15 + v0:15 + v1], T.cb[:, 528 + v0:528 + v1]
-        prev = "c0" if h == "a" else "cqa"
-        op("V", lambda: ts(T.high[:, v0:v1], T["pT" + h][:, 0:v1 - v0], -TH + 0.5, None, A.is_le), w=["high" + h], x=["pT" + h])
-        if between[0]:
-            between[0]()
-        op("V", lambda: V.tensor_tensor_scan(c, T.high[:, v0:v1], T[cap][:, v0:v1], T.cb[:, 15 + v0:16 + v0], A.add, A.min),
-           r=["high" + h, cap, prev], w=["cq" + h])
-        if between[1]:
-            between[1]()
-        op("V", lambda: V.tensor_tensor_scan(il, c, cp, 0.0, A.max, A.subtract), r=["cq" + h, prev], w=["ill" + h])
-        if between[2]:
-            between[2]()
-        names = ["blk%d%s" % (t, h)]
-        if h == "b":
-            op("V", lambda: ts(win[t][:, WB * q + P:WB * (q + 1)], T.cb[:, 520:528], float(-qo), None, A.add), r=["cqb"], w=["tail%d" % t])
-            names.append("tail%d" % t)
-        op("V", lambda: V.tensor_tensor_scan(win[t][:, WB * q + v0:WB * q + v1], il, nx(v0, v1), 0.0, A.max, A.mult),
-           r=["ill" + h, "nx" + h], w=names[:1])
-        allgather(win[t][:, WB * q + v0:WB * q + (v1 if h == "a" else WB)], names, "aw%d" % t, "win%d" % t)
-
-    def uninfected(t, nx):
-        qo = 8 * q if t < DAYS - 1 else 0
-        op("P", lambda: group([(T.pW[:, 0:64], Wr[r], T.cb[:, 16 + r:1040:16]) for r in range(16)]),
-           r=["Z", "cqa", "cqb", "illa", "illb"], x=["pW"])
-        op("V", lambda: ts(T.G[:, 8:2304:9], nx(0, 256), 8.0, 0.0, A.add, A.min), r=["nxa", "nxb"], w=["G8a"])
-        op("V", lambda: ts(T.pa[:], T.pW[:, 32:64], 1024.0, -512.0, A.mult, A.add), w=["pa"], x=["pW"])
-        op("V", lambda: ts(iw[t][:], T.pW[:, 32:64], 512.0, None, A.mult), w=["iw%d" % t], x=["pW"])
-        op("V", lambda: V.tensor_tensor(T.pb[:], T.pa[:], T.vc[:], A.max), r=["pa", "vc"], w=["pb"])
-        op("V", lambda: ts(T.G[:, 2312::9], nx(256, P), 8.0, 0.0, A.add, A.min), r=["nxa", "nxb"], w=["G8"])
-        op("V", lambda: V.tensor_tensor(T.pc[:], T.pb[:], T.pW[:, 0:32], A.subtract), r=["pb"], w=["pc"], x=["pW"])
-        op("V", lambda: ts(T.pos[:], T.pc[:], float(qo), None, A.add), r=["pc"], w=["pos"])
-        lb = ll[t][:, P * q:P * (q + 1)]
-        op("V", lambda: V.tensor_copy(lb.indirect(T.pos[:]), cq), r=["pos", "cqa", "cqb"], w=["lb%d" % t])
-        allgather(lb, ["lb%d" % t], "al%d" % t, "ll%d" % t)
-
-    def nx0(v0, v1):
-        return T.nx0[:, v0:v1]
-
-    def nxo(v0, v1):
-        return T.O[:, 9 * v0 + 8:9 * v1:9]
-
-    LN = ["L0", "L1", "L2"]
-    op("V", lambda: ts(T.nx0[:, 0:va], T.xi[:, 0:va], -1.0, None, A.mult), r=["xia"], w=["nxa"])
-    total("a", 0, va, nx0)
-    op("V", lambda: ts(T.nx0[:, va:P], T.xi[:, va:P], -1.0, None, A.mult), r=["xib"], w=["nxb"])
-    total("b", va, P, nx0)
-    infect(0, "a", 0, va, nx0, (
-        lambda: op("V", lambda: ts(T.pm[:, 0:1], T.pi[:, 0:1], 15, None, A.bitwise_and), r=["pi"], w=["pm0"]),
-        lambda: op("V", lambda: ts(T.Z[:, 15:128:16], T.B[:, 0:128:16], 1.0 / 16, None, A.mult), r=["B", "Z"], w=["Z"]),
-        lambda: op("V", lambda: V.tensor_copy(T.pf[:, 0:1], T.pm[:, 0:1]), r=["pm0"], w=["pf0"])))
-    infect(0, "b", va, P, nx0, (
-        lambda: op("V", lambda: ts(T.vc[:], T.i32[:], T.pf[:, 0:1], None, A.add), r=["pf0", "i32"], w=["vc"]),
-        lambda: op("V", lambda: V.tensor_copy(T.idh[:], T.idb[:]), r=["idb"], w=["idh"]), None))
-    fill("k512", 8, P)
-    op("V", lambda: ts(T.t1[:], T.nbi[:], 3584, None, A.bitwise_and), r=["nbi"], w=["t1"])
-    uninfected(0, nx0)
-    fill("capb", P, CAP)
-    fill("kneg", 128, -8 * UB)
-    fill("kpos", 128, 2048 + 8 * UB)
-    op("V", lambda: V.tensor_copy(T.rb[0:8, :], T.ri[0:8, :]), r=["ri"], w=["rb"])
-    op("V", lambda: ts(T.t2[:], T.t1[:], 1.0 / 64, -2048.0, A.mult, A.add), r=["t1"], w=["t2"])
-    op("P", lambda: PE.matmul(T.pTa[:], T.E[0:8, :], T.rb[0:8, :], True, True), r=["E", "rb"], x=["pTa"])
-    op("S", lambda: S.activation(T.D0[:, 8::9], T.pTa[:], AF.Copy), r=["D0a"], w=["D0a"], x=["pTa"])
-    op("V", lambda: ts(T.t3[:], T.d0[:], float(STEP), None, A.add), r=["d0"], w=["t3"])
-    op("V", lambda: V.tensor_tensor(T.L[:], T.t2[:], T.nbi[:], A.add), r=["t2", "nbi"], w=LN)
-    op("V", lambda: ts(T.d1[:], T.t3[:], 2047, None, A.bitwise_and), r=["t3"], w=["d1"])
-    op("V", lambda: ts(T.off[:], T.L[:], 2048.0, None, A.add), r=LN, w=["off", "off0"])
-    op("V", lambda: ts(T.t4[:], T.d0[:], float(2 * STEP), None, A.add), r=["d0"], w=["t4"])
-
-    for t in range(DAYS):
-        last = t == DAYS - 1
-        wn = ["win%d" % t, "blk%da" % t, "blk%db" % t, "tail%d" % t]
-        w = win[t][:]
-        tmn = ["jh", "idh", "idb"] + ["tm%d" % i for i in range(7)]
-        bounds = (0,) + SLA + (256,) if not last else (0, SLL[0], SLL[1], 256)
-        banks = ["pSa", "pSb", "pSc"]
-        pieces = [(banks[i], bounds[i], bounds[i + 1], T[banks[i]][:, 0:bounds[i + 1] - bounds[i]]) for i in range(3)]
-
-        def pick(e, out, src, r, names):
-            if e == "V":
-                op("V", lambda: V.tensor_copy(out, src), r=r, w=names)
-            else:
-                op("S", lambda: S.activation(out, src, AF.Copy), r=r, w=names)
-
-        def gather(e, k, c0, c1, names):
-            pick(e, T.G[:, 144 * c0 + k:144 * c1:9], w.indirect(T.off[:, 32 * k + c0:32 * k + c1]),
-                 wn + (["off0"] if 32 * k + c1 <= SLA[1] else ["off", "off0"]), names)
-
-        def slg(e, c0, c1, name):
-            pick(e, T.SG[:, 16 * c0:16 * c1], ll[t][:].indirect(T.idx[:, c0:c1]), ["ll%d" % t, "lb%d" % t, "idx"], [name])
-
-        def counts():
-            op("V", lambda: V.tensor_tensor_scan(T.C[:], T.k512[:], win[t][:, WB - 1::WB], 0.0, A.add, A.subtract), r=wn + ["k512"], w=["C"])
-            op("V", lambda: V.tensor_copy(T.nf[:], win[t][:, WB - 1::WB]), r=wn, w=["nf"])
-            op("V", lambda: ts(T.cs[:, 0:1], T.C[:, 7:8], 1.0 / 2048, None, A.mult), r=["C"], w=["cs"])
-
-        def place():
-            op("V", lambda: ts(T.ju[:], dd[t][:], T.cs[:, 0:1], -0.5 + 2.0 ** -12, A.mult, A.add), r=["cs", "d%d" % t], w=["ju"])
-
-        def index_terms(out, c0, c1):
-            return [(out, T.idh[:], T.jh[:, c0:c1])] + [(out, T.idb[:], T.tm[:, 256 * i + c0:256 * i + c1]) for i in range(7)]
-
-        def terms():
-            op("V", lambda: ts(T.jh[:], T.ju[:], -2048.0, None, A.add), r=["ju"], w=["jh"])
-            for i in range(7):
-                op("V", lambda: ts(T.tm[:, 256 * i:256 * (i + 1)], T.ju[:], T.C[:, i:i + 1], T.nf[:, i:i + 1], A.is_ge, A.mult),
-                   r=["ju", "C", "nf"], w=["tm%d" % i])
-            op("P", lambda: group(index_terms(T.pI[:, 0:256], 0, 256)), r=tmn, x=["pI"])
-
-        def offsets():
-            op("V", lambda: ts(T.idx[:], T.pI[:, 0:256], 2048.0, None, A.add), w=["idx"], x=["pI"])
-
-        def update(v0, v1, hs):
-            op("V", lambda: V.tensor_tensor_scan(T.O[:, 9 * v0:9 * v1], T.D0[:, 9 * v0:9 * v1], T.G[:, 9 * v0:9 * v1], 0.0, A.add, A.min),
-               r=["G%s%d" % (h, k) for k in range(8) for h in hs] + ["G8", "G8a", "D0a"], w=["nx" + h for h in hs])
-
-        def prewrap():
-            for bank, c0, c1, out in pieces:
-                mm = index_terms(out, c0, c1) + [(out, T.idf[:], T.L[:, c0:c1])]
-                if last:
-                    mm += [(out, T.idb[:], T.kneg[:, 0:c1 - c0]), (out, T.id8[:], T.ub[:, c0:c1])]
-                op("P", lambda: group(mm, stop=False), r=tmn + LN + ["idf", "kneg", "id8", "ub"], x=[bank])
-
-        def plain():
-            for c0 in (0, 128):
-                out = T.pW[:, 256 + c0:384 + c0]
-                op("P", lambda: group([(out, T.idp[:], T.L[:, c0:c0 + 128]), (out, T.idm8[:], T.ub[:, c0:c0 + 128]), (out, T.idb[:], T.kpos[:])]),
-                   r=LN + ["idp", "idm8", "ub", "kpos"], x=["pW"])
-
-        def wrap(i, names):
-            bank, c0, c1, out = pieces[i]
-            op("P", lambda: group([(out, Wr[r], T.SG[:, 16 * c0 + r:16 * c1:16]) for r in range(16)], start=False), r=["Z"] + names, x=[bank])
-
-        def select(i, step):
-            bank, c0, c1, out = pieces[i]
-            pw = T.pW[:, 256 + c0:256 + c1]
-            if step == 0:
-                op("V", lambda: V.tensor_tensor(T.dl[:, c0:c1] if last else pw, out, T.h[:, c0:c1], A.mult), r=["h"], w=["dl%d" % i],
-                   x=[bank] + ([] if last else ["pW"]))
-            elif last:
-                op("V", lambda: V.tensor_tensor(T.ynbs[:, c0:c1], pw, T.dl[:, c0:c1], A.add), r=["dl%d" % i], w=["yn%d" % i], x=["pW"])
-                op("Y", lambda: SY.dma_start(T.ynb[:, c0:c1], T.ynbs[:, c0:c1]), r=["yn%d" % i], sem="stn%d" % i)
-            else:
-                op("V", lambda: V.tensor_tensor(T.L[:, c0:c1], pw, T.L[:, c0:c1], A.add), r=["dl%d" % i], w=[LN[i]], x=["pW"])
-
-        def hit():
-            op("V", lambda: ts(T.h[:], T.pF[:, 0:256], -30.0, None, A.is_lt), w=["h"], x=["pF"])
-
-        if not last:
-            ca = CA[t + 1]
-            va = 16 * ca
-            for k in range(7):
-                gather("S", k, 0, ca, ["Ga%d" % k])
-            for k in range(6):
-                gather("S", k, ca, 32, ["Gb%d" % k])
-            counts()
-            gather("V", 7, 0, 32, ["Ga7", "Gb7"])
-            place()
-            gather("V", 6, ca, 32, ["Gb6"])
-            flags(t, [7])
-            rest = [6, 0, 1, 2, 3, 4, 5]
-            terms()
-            update(0, va, "a")
-            total("a", 0, va, nxo)
-            offsets()
-            if t == DAYS - 2:
-                op("V", lambda: V.memset(T.cb[:, 0:16], 0.0), w=["c0"])
-            infect(t + 1, "a", 0, va, nxo)
-            update(va, P, "b")
-            flags(t, rest[:FPRE])
-            total("b", va, P, nxo)
-            if t == 0:
-                op("V", lambda: ts(T.d2[:], T.t4[:], 2047, None, A.bitwise_and), r=["t4"], w=["d2"])
-            for i in range(3):
-                slg("S", bounds[i], bounds[i + 1], "SG%d" % i)
-            flags(t, rest[FPRE:FPRE + FMID])
-            infect(t + 1, "b", va, P, nxo)
-            uninfected(t + 1, nxo)
-            flags(t, rest[FPRE + FMID:])
-            prewrap()
-            for i in range(3):
-                wrap(i, ["SG%d" % i])
-            hit()
-            for i, step in ((0, 0), (1, 0), (0, 1), (1, 1)):
-                select(i, step)
-            op("V", lambda: ts(T.off[:, 0:SLA[1]], T.L[:, 0:SLA[1]], 2048.0, None, A.add), r=LN[:2], w=["off0"])
-            select(2, 0)
-            select(2, 1)
-            op("V", lambda: ts(T.off[:, SLA[1]:], T.L[:, SLA[1]:], 2048.0, None, A.add), r=LN[2:], w=["off"])
-        else:
-            for k in range(6):
-                gather("S", k, 0, 32, ["Ga%d" % k, "Gb%d" % k])
-            counts()
-            op("V", lambda: ts(T.ub[:], T.L[:], 1.0 / WB, UB + 2048.0 / WB - 0.492, A.mult, A.add), r=LN, w=["ub"])
-            place()
-            plain()
-            flags(t, [0, 1])
-            terms()
-            gather("V", 7, 0, 32, ["Ga7", "Gb7"])
-            offsets()
-            gather("V", 6, 0, 32, ["Ga6", "Gb6"])
-            flags(t, [2, 7, 3, 4, 6, 5])
-            prewrap()
-            a, b, c = SLL
-            slg("S", 0, a, "SG0")
-            update(0, P, "ab")
-            slg("V", a, b, "SG1")
-            op("S", lambda: S.activation(T.yxs[:], T.O[:, 8::9], AF.Copy, scale=-1.0), r=["nxa", "nxb"], w=["yxs"])
-            op("Y", lambda: SY.dma_start(T.yx[:], T.yxs[:]), r=["yxs"], sem="sty")
-            slg("S", b, c, "SG2")
-            hit()
-            slg("V", c, 256, "SG3")
-            wrap(0, ["SG0"])
-            wrap(1, ["SG1"])
-            wrap(2, ["SG2", "SG3"])
-            for i, step in ((0, 0), (1, 0), (0, 1), (1, 1), (2, 0), (2, 1)):
-                select(i, step)
+    first = sending(0, nx0)
+    first.update({
+        "nxa": vop(lambda: ts(T.nx0[:, 0:va], T.xi[:, 0:va], -1.0, None, A.mult), r=["xia"], w=["nxa"]),
+        "nxb": vop(lambda: ts(T.nx0[:, va:P], T.xi[:, va:P], -1.0, None, A.mult), r=["xib"], w=["nxb"]),
+        "pm": vop(lambda: ts(T.pm[:, 0:1], T.pi[:, 0:1], 15, None, A.bitwise_and), r=["pi"], w=["pm0"]),
+        "Z": vop(lambda: ts(T.Z[:, 15:128:16], T.B[:, 0:128:16], 1.0 / 16, None, A.mult), r=["B", "Z"], w=["Z"]),
+        "pf": vop(lambda: V.tensor_copy(T.pf[:, 0:1], T.pm[:, 0:1]), r=["pm0"], w=["pf0"]),
+        "vc": vop(lambda: ts(T.vc[:], T.i32[:], T.pf[:, 0:1], None, A.add), r=["pf0", "i32"], w=["vc"]),
+        "idh": vop(lambda: V.tensor_copy(T.idh[:], T.idb[:]), r=["idb"], w=["idh"]),
+        "k512": fill("k512", 8, P), "kneg": fill("kneg", 128, -8 * UB), "kpos": fill("kpos", 128, 2048 + 8 * UB),
+        "rb": vop(lambda: V.tensor_copy(T.rb[0:8, :], T.ri[0:8, :]), r=["ri"], w=["rb"]),
+        "res": resist,
+        "t1": vop(lambda: ts(T.t1[:], T.nbi[:], 3584, None, A.bitwise_and), r=["nbi"], w=["t1"]),
+        "t2": vop(lambda: ts(T.t2[:], T.t1[:], 1.0 / 64, -2048.0, A.mult, A.add), r=["t1"], w=["t2"]),
+        "L": vop(lambda: V.tensor_tensor(T.L[:], T.t2[:], T.nbi[:], A.add), r=["t2", "nbi"], w=LN),
+        "off": vop(lambda: ts(T.off[:], T.L[:], 2048.0, None, A.add), r=LN, w=["off0", "off1", "off2"]),
+        "t3": vop(lambda: ts(T.t3[:], T.d0[:], float(STEP), None, A.add), r=["d0"], w=["t3"]),
+        "d1": vop(lambda: ts(T.d1[:], T.t3[:], 2047, None, A.bitwise_and), r=["t3"], w=["d1"]),
+        "t4": vop(lambda: ts(T.t4[:], T.d0[:], float(2 * STEP), None, A.add), r=["d0"], w=["t4"]),
+        "d2": vop(lambda: ts(T.d2[:], T.t4[:], 2047, None, A.bitwise_and), r=["t4"], w=["d2"]),
+    })
+    for steps, order in ((first, START), (daily(0), DAY), (daily(1), DAY), (daily(2), LAST)):
+        for name in order.split():
+            steps[name]()
 
     g.wait_ge(T.sem.sent, sent["sent"])
-    for s in ("cV", "cS", "cP", "cG"):
+    for s in ("cV", "cS", "cP", "cG", "sty", "stn0", "stn1", "stn2"):
         SY.wait_ge(T.sem[s], count[s])
-    for s in ("sty", "stn0", "stn1", "stn2"):
-        SY.wait_ge(T.sem[s], 16)

@@ -20,12 +20,13 @@ SCRATCH = {
     "ones": sb(128, BF), "B1": sb(128, BF), "B": sb(128, BF), "idb": sb(128, BF), "idh": sb(128, F16), "idf": sb(128, F32),
     "id8": sb(128, BF), "idm8": sb(128, BF), "idp": sb(128, F32),
     "E": sb(128, BF), "Z": sb(144, BF), "kneg": sb(128, BF), "kpos": sb(128, BF),
-    "high": sb(512, BF), "cb": sb(1040, BF), "cap": sb(512, BF), "kq": sb(512, BF),
+    "high": sb(512, BF), "cb": sb(1040, BF), "cap": sb(512, BF), "dig": sb(512, BF), "dign": sb(512, BF),
+    "lo": sb(64, BF), "i8": sb(8, F32), "bc": sb(8, F32), "bcn": sb(8, F32), "Z2": sb(144, BF), "ids": sb(128, BF),
     "pi": sb(8, I32), "pm": sb(8, I32), "pf": sb(8, F32), "i32": sb(32, I32), "vc": sb(32, F32),
     "pa0": sb(32, BF), "pa1": sb(32, BF), "pa2": sb(32, BF), "pb": sb(32, F32), "pc": sb(32, F32), "pos": sb(32, U16),
     "k512": sb(8, F32), "C": sb(8, F32), "cs": sb(8, F32), "nf": sb(8, F32),
     "t1": sb(256, I32), "t2": sb(256, F32), "t3": sb(256, I32), "t4": sb(256, I32), "d1": sb(256, I32), "d2": sb(256, I32),
-    "L": sb(256, F32), "off": sb(256, U16), "ju": sb(256, U16), "jh": sb(256, F16), "ih": sb(256, F16), "tm": sb(7 * 256, BF),
+    "L": sb(256, F32), "off": sb(256, U16), "ju": sb(256, U16), "jh": sb(256, F16), "tm": sb(3 * 256, F16),
     "idx": sb(256, U16), "h": sb(256, F32), "ub": sb(256, BF), "Lf": sb(256, F32), "yxs": sb(512, F32), "ynbs": sb(256, F32),
 }
 for _n in ("pTa", "pTb", "pW", "pF", "pI", "pSa", "pSb", "pSc"):
@@ -33,16 +34,12 @@ for _n in ("pTa", "pTb", "pW", "pF", "pI", "pSa", "pSb", "pSc"):
 SEMAPHORES = ["cV", "cS", "cP", "cG", "ldxa", "ldxb", "ldn", "ldd", "ldr", "sty", "stn0", "stn1", "stn2", "sent",
               "aw0", "aw1", "aw2", "al0", "al1", "al2"]
 
-CA = [8, 16, 16]
+CA = [12, 12, 12]
 SLA = (0, 128, 192, 256)
 
-START = """nxa ta ia0 ia1 g8a ia2 ia3 Z t1 nxb t2 t4 tb pm ib0 rb ib1 pf ib4 ib2 vc ib3 pw idh d2 L res pa g8b pb t3 off kneg pc
-kpos k512 d1 pos scat"""
-DAY = """C a5S a1V cs nf a4S a6V ju b6V a2V a7S t5 b7S t4 t2 t6 t0 jh a0S t3 f7 a3S b3S f6 t1 p0 ua x0 p1 b2S p2 b1V b5S ta f2 f1
-b4S b0S ia0 f4 x1 x2 ia1 ub ia2 f3 ih tb s2S ia3 ib0 f5 g8b ib1 f0 ib2 ib4 s3V s5S pw pa l1 s4S w1 ib3 s0S l2 s1S pb h0 l0 h1
-s7S pc g8a w0 m1 s6S w2 pos h2 n1 scat m0 o1 m2 n0 n2 o0 o2"""
-LAST = """C blk plain c0S cs nf ju t2 t6 t5 f0 c1S t0 c3S t1 t4 f1 jh t3 c5V c7V p1 p0 x0 p2 f5 c2S c4S x1 c6V x2 f7 s4V f2 ih u
-f6 l0 l2 f3 f4 s5V s2S s7V l1 s1S h0 h1 s0S h2 s3S w0 yx m0 w1 s6S m1 n0 n1 w2 m2 n2"""
+START = """nxa idb ta ia0 Da i8 i32 pm ia3 idp kpos nxb pm1 rb pf tb lo Z ib0 ia1 idf kneg t1 ib1 t4 E Db ib2 pw ev ib4 g8a t2 idm8 vc bcn ib3 g8b wc bc t3 Z2 pa L pb Dc idh pc dign d1 pos dig k512 id8 off d2 ids scat res"""
+DAY = """b5V c4S ^w2 ^m2 a1S C a5S f4 c0V nf ^n2 cs a2V ^o2 ju c3S f3 c6V t0 c7S t2 b1S t1 jh f0 ua b2S p1 p0 x1 s5S ub f1 ta l1 ia0 f5 x0 f6 ia3 s4S tb ia1 ib0 f2 f7 p2 g8b ib1 ib2 ib4 x2 h0 pw l2 ib3 g8a s13S h2 pa h1 w1 l0 pb pc m1 s0S pos w0 n1 s7S scat m0 s6S o1 n0 o0"""
+LAST = """^w2 C c4S c5V cs nf ^m2 f4 c2S ju ^n2 c3S c0V c1S t1 f5 jh f2 f3 ^o2 c6S t2 t0 p0 p1 f0 f1 c7V x0 p2 blk s3V s12S s0V x1 f7 s45S x2 u f6 l2 l0 s7S s6V plain l1 h0 h1 w0 w1 h2 m0 m1 yx w2 n0 n1 m2 n2"""
 
 
 def rank_program(g, core, T, topo):
@@ -121,7 +118,7 @@ def rank_program(g, core, T, topo):
     dd = [T.d0, T.d1, T.d2]
     pa = [T.pa0, T.pa1, T.pa2]
     Wr = [T.Z[:, 15 - r:143 - r] for r in range(16)]
-    cq = T.cb[:, 16:528]
+    Wd = [T.Z2[:, 15 - r:143 - r] for r in range(16)]
     LN = ["L0", "L1", "L2"]
     banks = ["pSa", "pSb", "pSc"]
     pieces = [(banks[i], SLA[i], SLA[i + 1], T[banks[i]][:, 0:SLA[i + 1] - SLA[i]]) for i in range(3)]
@@ -142,9 +139,10 @@ def rank_program(g, core, T, topo):
                 c, cp, il = T.cb[:, 16 + v0:16 + v1], T.cb[:, 15 + v0:15 + v1], T.cb[:, 528 + v0:528 + v1]
                 prev, bank, blk = "c0" if h == "a" else "cqa", "pT" + h, "blk%d%s" % (t, h)
                 step["t" + h] = pop(lambda: PE.matmul(T[bank][:, 0:v1 - v0], T.B[:], nx(v0, v1), True, True), r=["B", "nx" + h], x=[bank])
-                step["i%s0" % h] = vop(lambda: ts(T.high[:, v0:v1], T[bank][:, 0:v1 - v0], -TH + 0.5, None, A.is_le), w=["high" + h], x=[bank])
-                step["i%s1" % h] = vop(lambda: V.tensor_tensor_scan(c, T.high[:, v0:v1], T.cap[:, v0:v1], T.cb[:, 15 + v0:16 + v0], A.add, A.min),
-                                       r=["high" + h, "cap", prev], w=["cq" + h])
+                high, hn = (il, "ill" + h) if v1 <= CAP else (T.high[:, v0:v1], "high" + h)
+                step["i%s0" % h] = vop(lambda: ts(high, T[bank][:, 0:v1 - v0], -TH + 0.5, None, A.is_le), w=[hn], x=[bank])
+                step["i%s1" % h] = vop(lambda: V.tensor_tensor_scan(c, high, T.cap[:, v0:v1], T.cb[:, 15 + v0:16 + v0], A.add, A.min),
+                                       r=[hn, "cap", prev], w=["cq" + h])
                 step["i%s2" % h] = vop(lambda: V.tensor_tensor_scan(il, c, cp, 0.0, A.max, A.subtract), r=["cq" + h, prev], w=["ill" + h])
 
                 def send():
@@ -158,17 +156,15 @@ def rank_program(g, core, T, topo):
                          r=["Z", "cqa", "cqb", "illa", "illb"], x=["pW"])
         step["g8a"] = vop(lambda: ts(T.G[:, 8:9 * va:9], nx(0, va), 8.0, 0.0, A.add, A.min), r=["nxa"], w=["G8a"])
         step["g8b"] = vop(lambda: ts(T.G[:, 9 * va + 8::9], nx(va, P), 8.0, 0.0, A.add, A.min), r=["nxb"], w=["G8b"])
-        step["pa"] = vop(lambda: ts(pa[t][:], T.pW[:, 32:64], 1024.0, -512.0, A.mult, A.add), w=["pa%d" % t], x=["pW"])
-        step["pb"] = vop(lambda: V.tensor_tensor(T.pb[:], pa[t][:], T.vc[:], A.max), r=["pa%d" % t, "vc"], w=["pb"])
+        odd = q % 2
+        step["pa"] = vop(lambda: ts(pa[t][:], T.pW[:, 32:64], 512.0 if odd else -512.0, 0.0 if odd else 512.0, A.mult, A.add), w=["pa%d" % t], x=["pW"])
+        step["pb"] = vop(lambda: V.tensor_tensor(T.pb[:], pa[t][:], T.vc[:], A.max if odd else A.min), r=["pa%d" % t, "vc"], w=["pb"])
         step["pc"] = vop(lambda: V.tensor_tensor(T.pc[:], T.pb[:], T.pW[:, 0:32], A.subtract), r=["pb"], w=["pc"], x=["pW"])
-        step["pos"] = vop(lambda: V.tensor_copy(T.pos[:], T.pc[:]), r=["pc"], w=["pos"])
+        step["pos"] = vop(lambda: ts(T.pos[:], T.pc[:], 0.0 if odd else T.cb[:, 527:528], None, A.add), r=["pc", "cqb"], w=["pos"])
 
         def scatter():
-            lb = ll[t][:, P * q:P * (q + 1)]
-            if t < DAYS - 1:
-                op("V", lambda: V.tensor_tensor(lb.indirect(T.pos[:]), cq, T.kq[:], A.add), r=["pos", "cqa", "cqb", "kq"], w=["lb%d" % t])
-            else:
-                op("V", lambda: V.tensor_copy(lb.indirect(T.pos[:]), cq), r=["pos", "cqa", "cqb"], w=["lb%d" % t])
+            lb, dig = ll[t][:, P * q:P * (q + 1)], "dig" if t < DAYS - 1 else "dign"
+            op("V", lambda: V.tensor_copy(lb.indirect(T.pos[:]), T[dig][:]), r=["pos", dig], w=["lb%d" % t])
             allgather(lb, ["lb%d" % t], "al%d" % t, "ll%d" % t)
         step["scat"] = scatter
         return step
@@ -196,13 +192,15 @@ def rank_program(g, core, T, topo):
                 for h, c0, c1, hs in (("a", 0, ca, "a"), ("b", ca, 32, "b"), ("c", 0, 32, "ab")):
                     step["%s%d%s" % (h, k, e)] = pick(e, T.G[:, 144 * c0 + k:144 * c1:9], win[t][:].indirect(T.off[:, 32 * k + c0:32 * k + c1]),
                                                       wn + ["off%d" % i], ["G%s%d" % (x, k) for x in hs])
-                step["s%d%s" % (k, e)] = pick(e, T.SG[:, 512 * k:512 * k + 512], ll[t][:].indirect(T.idx[:, 32 * k:32 * k + 32]),
-                                              ["ll%d" % t, "lb%d" % t, "idx%d" % i], ["SG%d" % k])
+                for k1 in range(k, 8):
+                    step["s%d%s%s" % (k, k1 if k1 > k else "", e)] = pick(
+                        e, T.SG[:, 512 * k:512 * k1 + 512], ll[t][:].indirect(T.idx[:, 32 * k:32 * k1 + 32]),
+                        ["ll%d" % t, "lb%d" % t] + ["idx%d" % j for j in range(i, 3) if SLA[j] <= 32 * k1], ["SG%d" % j for j in range(k, k1 + 1)])
 
             def flags(k=k):
                 out = T.pF[:, 32 * k:32 * k + 32]
-                mm = [(out, Wr[r], T.G[:, 9 * r + k::144]) for r in range(16)] + [(out, T.idb[:], pa[t][:])]
-                op("P", lambda: group(mm), r=["Z", "idb", "pa%d" % t, "Ga%d" % k, "Gb%d" % k], w=["F%d" % k], x=["pF"])
+                mm = [(out, Wr[r], T.G[:, 9 * r + k::144]) for r in range(16)] + [(out, T.ids[:], pa[t][:])]
+                op("P", lambda: group(mm), r=["Z", "ids", "pa%d" % t, "Ga%d" % k, "Gb%d" % k], w=["F%d" % k], x=["pF"])
             step["f%d" % k] = flags
         for name, v0, v1, hs in (("ua", 0, 16 * ca, "a"), ("ub", 16 * ca, P, "b"), ("u", 0, P, "ab")):
             step[name] = vop(lambda v0=v0, v1=v1: V.tensor_tensor_scan(T.O[:, 9 * v0:9 * v1], T.D0[:, 9 * v0:9 * v1], T.G[:, 9 * v0:9 * v1], 0.0, A.add, A.min),
@@ -210,25 +208,24 @@ def rank_program(g, core, T, topo):
         step["C"] = vop(lambda: V.tensor_tensor_scan(T.C[:], T.k512[:], nf, 0.0, A.add, A.subtract), r=wn + ["k512"], w=["C"])
         step["cs"] = vop(lambda: ts(T.cs[:, 0:1], T.C[:, 7:8], 1.0 / 2048, None, A.mult), r=["C"], w=["cs"])
         step["ju"] = vop(lambda: ts(T.ju[:], dd[t][:], T.cs[:, 0:1], -0.5 + 2.0 ** -12, A.mult, A.add), r=["cs", "d%d" % t], w=["ju"])
-        step["jh"] = vop(lambda: ts(T.jh[:], T.ju[:], -2048.0, None, A.add), r=["ju"], w=["jh"])
-        step["ih"] = vop(lambda: ts(T.ih[:], T.idx[:], -2048.0, None, A.add), r=["idx0", "idx1", "idx2"], w=["ih"])
-        for i in range(7):
-            step["t%d" % i] = vop(lambda i=i: ts(T.tm[:, 256 * i:256 * (i + 1)], T.ju[:], T.C[:, i:i + 1], T.nf[:, i:i + 1], A.is_ge, A.mult),
+        step["jh"] = vop(lambda: ts(T.jh[:], T.ju[:], nf[:, 0:1], -2048.0, A.add, A.add), r=["ju"] + wn, w=["jh"])
+        for i in range(3):
+            step["t%d" % i] = vop(lambda i=i: ts(T.tm[:, 256 * i:256 * (i + 1)], T.ju[:], T.C[:, 2 * i + 1:2 * i + 2], T.nf[:, i:i + 1], A.is_ge, A.mult),
                                   r=["ju", "C", "nf"], w=["tm%d" % i])
-        step["nf"] = vop(lambda: V.tensor_copy(T.nf[:], nf), r=wn, w=["nf"])
+        step["nf"] = vop(lambda: V.tensor_tensor(T.nf[:, 0:3], nf[:, 1:6:2], nf[:, 2:7:2], A.add), r=wn, w=["nf"])
         for i, (bank, c0, c1, out) in enumerate(pieces):
             def piece(i=i, bank=bank, c0=c0, c1=c1, out=out):
                 ks = range(c0 // 32, c1 // 32)
-                mm = [(out, T.idh[:], T.jh[:, c0:c1])] + [(out, T.idb[:], T.tm[:, 256 * j + c0:256 * j + c1]) for j in range(7)]
-                step["p%d" % i] = pop(lambda: group(mm), r=["jh", "idh", "idb"] + ["tm%d" % j for j in range(7)], x=[bank])
+                mm = [(out, T.idh[:], T.jh[:, c0:c1])] + [(out, T.idh[:], T.tm[:, 256 * j + c0:256 * j + c1]) for j in range(3)]
+                step["p%d" % i] = pop(lambda: group(mm), r=["jh", "idh"] + ["tm%d" % j for j in range(3)], x=[bank])
                 step["x%d" % i] = vop(lambda: ts(T.idx[:, c0:c1], out, 2048.0, None, A.add), w=["idx%d" % i], x=[bank])
-                ml = [(out, T.idh[:], T.ih[:, c0:c1]), (out, T.idf[:], T.L[:, c0:c1])]
+                ml = [(out, T.idf[:], T.L[:, c0:c1])]
                 if last:
                     ml += [(out, T.idb[:], T.kneg[:, 0:c1 - c0]), (out, T.id8[:], T.ub[:, c0:c1])]
-                step["l%d" % i] = pop(lambda: group(ml, stop=False), r=[LN[i], "ih", "idf", "kneg", "id8", "ub"], x=[bank])
-                step["w%d" % i] = pop(lambda: group([(out, Wr[r], T.SG[:, 16 * c0 + r:16 * c1:16]) for r in range(16)], start=False),
-                                      r=["Z"] + ["SG%d" % k for k in ks], x=[bank])
-                step["h%d" % i] = vop(lambda: ts(T.h[:, c0:c1], T.pF[:, c0:c1], -542.0, None, A.is_lt), r=["F%d" % k for k in ks], w=["h%d" % i], x=["pF"])
+                step["l%d" % i] = pop(lambda: group(ml, stop=False), r=[LN[i], "idf", "kneg", "id8", "ub"], x=[bank])
+                step["w%d" % i] = pop(lambda: group([(out, Wd[r], T.SG[:, 16 * c0 + r:16 * c1:16]) for r in range(16)], start=False),
+                                      r=["Z2"] + ["SG%d" % k for k in ks], x=[bank])
+                step["h%d" % i] = vop(lambda: ts(T.h[:, c0:c1], T.pF[:, c0:c1], -30.0 if q % 2 else -542.0, None, A.is_lt), r=["F%d" % k for k in ks], w=["h%d" % i], x=["pF"])
                 pw = T.pI[:, 256 + c0:256 + c1]
                 if last:
                     step["m%d" % i] = vop(lambda: V.tensor_tensor(T.Lf[:, c0:c1], out, T.h[:, c0:c1], A.mult), r=["h%d" % i], w=["dl%d" % i], x=[bank])
@@ -240,9 +237,9 @@ def rank_program(g, core, T, topo):
                 else:
                     step["m%d" % i] = vop(lambda: V.tensor_tensor(pw, out, T.h[:, c0:c1], A.mult), r=["h%d" % i], w=["dl%d" % i], x=[bank, "pI"])
                     step["n%d" % i] = vop(lambda: V.tensor_tensor(T.L[:, c0:c1], pw, T.L[:, c0:c1], A.add), r=["dl%d" % i], w=[LN[i]], x=["pI"])
-                    step["o%d" % i] = vop(lambda: ts(T.off[:, c0:c1], T.L[:, c0:c1], 2048.0, None, A.add), r=[LN[i]], w=["off%d" % i])
+                    step["o%d" % i] = vop(lambda: V.tensor_copy(T.off[:, c0:c1], T.L[:, c0:c1]), r=[LN[i]], w=["off%d" % i])
             piece()
-        step["blk"] = vop(lambda: ts(T.ub[:], T.L[:], 1.0 / WB, UB + 2048.0 / WB - 0.492, A.mult, A.add), r=LN, w=["ub"])
+        step["blk"] = vop(lambda: ts(T.ub[:], T.L[:], 1.0 / WB, UB - 0.492, A.mult, A.add), r=LN, w=["ub"])
 
         def plain():
             for c0 in (0, 128):
@@ -271,17 +268,26 @@ def rank_program(g, core, T, topo):
     op("V", lambda: V.memset(T.cb[:, 0:16], 0.0), w=["c0"])
     op("V", lambda: V.memset(T.D0[:, 0:576:9], 512.0), r=["D0a"], w=["D0a"])
     op("V", lambda: V.memset(T.Z[:], 0.0), w=["Z"])
-    op("V", lambda: V.memset(T.kq[:], float((WB - P) * q)), w=["kq"])
+    op("V", lambda: V.memset(T.Z2[:], 0.0), w=["Z2"])
     op("G", lambda: g.affine_select(T.B1[:], T.ones[:], [[-16, 8], [0, 16]], A.is_ge, 0.0, 0, 1), r=["ones"], w=["B1"])
     op("G", lambda: g.affine_select(T.B[:], T.B1[:], [[16, 8], [0, 16]], A.is_ge, 0.0, 15, -1), r=["B1"], w=["B"])
     op("G", lambda: g.iota(T.pi[:], [[0, 8]], 0, 1), w=["pi"])
-    op("G", lambda: g.iota(T.i32[:], [[16, 32]], 0, 0), w=["i32"])
-    op("G", lambda: g.affine_select(T.idb[:], T.ones[:], [[-1, 128]], A.is_equal, 0.0, 0, 1), r=["ones"], w=["idb"])
-    op("G", lambda: g.affine_select(T.E[0:8, :], T.ones[0:8, :], [[-1, 8], [0, 16]], A.is_equal, 0.0, 0, 1), r=["ones"], w=["E"])
-    for n in (576, 1152, 2304):
-        op("S", lambda: S.activation(T.D0[:, n:2 * n], T.D0[:, 0:n], AF.Copy), r=["D0a"], w=["D0a"])
-    for name, f in (("idf", -1.0), ("id8", 8.0), ("idm8", -8.0), ("idp", 1.0)):
-        op("S", lambda: S.activation(T[name][:], T.idb[:], AF.Copy, scale=f), r=["idb"], w=[name])
+
+    def ramp(name, n, step):
+        return lambda: op("G", lambda: g.iota(T[name][:], [[step, n]], 0, 0, allow_small_or_imprecise_dtypes=True), w=[name])
+
+    def double(n):
+        return lambda: op("S", lambda: S.activation(T.D0[:, n:2 * n], T.D0[:, 0:n], AF.Copy), r=["D0a"], w=["D0a"])
+
+    def scaled(name, f):
+        return lambda: op("S", lambda: S.activation(T[name][:], T.idb[:], AF.Copy, scale=f), r=["idb"], w=[name])
+
+    def digits(name, bias):
+        def run():
+            for c in range(8):
+                op("S", lambda: S.activation(T[name][:, 64 * c:64 * c + 64], T.lo[:], AF.Identity, bias=T[bias][:, c:c + 1], scale=T.pf[:, 1:2]),
+                   r=["lo", bias, "pf0"], w=[name + str(c)] if c < 7 else [name])
+        return run
 
     def resist():
         op("P", lambda: PE.matmul(T.pTa[:], T.E[0:8, :], T.rb[0:8, :], True, True), r=["E", "rb"], x=["pTa"])
@@ -293,24 +299,42 @@ def rank_program(g, core, T, topo):
         "nxb": vop(lambda: ts(T.nx0[:, va:P], T.xi[:, va:P], -1.0, None, A.mult), r=["xib"], w=["nxb"]),
         "pm": vop(lambda: ts(T.pm[:, 0:1], T.pi[:, 0:1], 15, None, A.bitwise_and), r=["pi"], w=["pm0"]),
         "Z": vop(lambda: ts(T.Z[:, 15:128:16], T.B[:, 0:128:16], 1.0 / 16, None, A.mult), r=["B", "Z"], w=["Z"]),
-        "pf": vop(lambda: V.tensor_copy(T.pf[:, 0:1], T.pm[:, 0:1]), r=["pm0"], w=["pf0"]),
+        "pm1": vop(lambda: ts(T.pm[:, 1:2], T.pi[:, 1:2], 1, None, A.bitwise_and), r=["pi"], w=["pm1"]),
+        "pf": vop(lambda: V.tensor_copy(T.pf[:, 0:2], T.pm[:, 0:2]), r=["pm0", "pm1"], w=["pf0"]),
+        "ev": vop(lambda: ts(T.pf[:, 2:3], T.pm[:, 1:2], -1.0, 1.0, A.mult, A.add), r=["pm1"], w=["ev"]),
+        "wc": vop(lambda: ts(T.pf[:, 3:4], T.pm[:, 1:2], 1.0 / 8 - 8, 8.0, A.mult, A.add), r=["pm1"], w=["wc"]),
+        "Z2": vop(lambda: ts(T.Z2[:, 15:128:16], T.B[:, 0:128:16], T.pf[:, 3:4], None, A.mult), r=["B", "Z2", "wc"], w=["Z2"]),
+        "bc": vop(lambda: ts(T.bc[:], T.i8[:], T.pf[:, 2:3], 8.0 * q, A.mult, A.add), r=["i8", "ev"], w=["bc"]),
+        "bcn": vop(lambda: ts(T.bcn[:], T.i8[:], 8.0 * q, T.pf[:, 2:3], A.add, A.mult), r=["i8", "ev"], w=["bcn"]),
+        "dig": digits("dig", "bc"), "dign": digits("dign", "bcn"),
+        "i32": ramp("i32", 32, 16), "i8": ramp("i8", 8, 1), "lo": ramp("lo", 64, 1),
+        "idb": lambda: op("G", lambda: g.affine_select(T.idb[:], T.ones[:], [[-1, 128]], A.is_equal, 0.0, 0, 1), r=["ones"], w=["idb"]),
+        "E": lambda: op("G", lambda: g.affine_select(T.E[0:8, :], T.ones[0:8, :], [[-1, 8], [0, 16]], A.is_equal, 0.0, 0, 1), r=["ones"], w=["E"]),
+        "Da": double(576), "Db": double(1152), "Dc": double(2304),
+        "idf": scaled("idf", -1.0), "id8": scaled("id8", 8.0), "idm8": scaled("idm8", -8.0), "idp": scaled("idp", 1.0),
+        "ids": scaled("ids", 1.0 if q % 2 else -1.0),
         "vc": vop(lambda: ts(T.vc[:], T.i32[:], T.pf[:, 0:1], None, A.add), r=["pf0", "i32"], w=["vc"]),
         "idh": vop(lambda: V.tensor_copy(T.idh[:], T.idb[:]), r=["idb"], w=["idh"]),
-        "k512": fill("k512", 8, P), "kneg": fill("kneg", 128, -8 * UB), "kpos": fill("kpos", 128, 2048 + 8 * UB),
+        "k512": fill("k512", 8, P), "kneg": fill("kneg", 128, -8 * UB), "kpos": fill("kpos", 128, 8 * UB),
         "rb": vop(lambda: V.tensor_copy(T.rb[0:8, :], T.ri[0:8, :]), r=["ri"], w=["rb"]),
         "res": resist,
         "t1": vop(lambda: ts(T.t1[:], T.nbi[:], 3584, None, A.bitwise_and), r=["nbi"], w=["t1"]),
-        "t2": vop(lambda: ts(T.t2[:], T.t1[:], 1.0 / 64, -2048.0, A.mult, A.add), r=["t1"], w=["t2"]),
+        "t2": vop(lambda: ts(T.t2[:], T.t1[:], 1.0 / 64, None, A.mult), r=["t1"], w=["t2"]),
         "L": vop(lambda: V.tensor_tensor(T.L[:], T.t2[:], T.nbi[:], A.add), r=["t2", "nbi"], w=LN),
-        "off": vop(lambda: ts(T.off[:], T.L[:], 2048.0, None, A.add), r=LN, w=["off0", "off1", "off2"]),
+        "off": vop(lambda: V.tensor_copy(T.off[:], T.L[:]), r=LN, w=["off0", "off1", "off2"]),
         "t3": vop(lambda: ts(T.t3[:], T.d0[:], float(STEP), None, A.add), r=["d0"], w=["t3"]),
         "d1": vop(lambda: ts(T.d1[:], T.t3[:], 2047, None, A.bitwise_and), r=["t3"], w=["d1"]),
         "t4": vop(lambda: ts(T.t4[:], T.d0[:], float(2 * STEP), None, A.add), r=["d0"], w=["t4"]),
         "d2": vop(lambda: ts(T.d2[:], T.t4[:], 2047, None, A.bitwise_and), r=["t4"], w=["d2"]),
     })
+    before = {}
     for steps, order in ((first, START), (daily(0), DAY), (daily(1), DAY), (daily(2), LAST)):
         for name in order.split():
-            steps[name]()
+            if name[0] != "^":
+                steps[name]()
+            elif name[1:] in before:
+                before[name[1:]]()
+        before = steps if steps is not first else {}
 
     g.wait_ge(T.sem.sent, sent["sent"])
     for s in ("cV", "cS", "cP", "cG", "sty", "stn0", "stn1", "stn2"):

from concourse.bass import DstId, RemoteDMATransfer
from concourse.mybir import AluOpType as A, ActivationFunctionType as AF

P, NR, DAYS = 512, 8, 3
WB = 520
CAP, TH, STEP = 192, 960, 77
UB = 136


def sb(cols, dtype):
    return ("sbuf", [128, cols], dtype)


BF, F32, I32, U16, F16 = "bfloat16", "float32", "int32", "uint16", "float16"
SCRATCH = {
    "xi": sb(512, I32), "nbi": sb(256, I32), "d0": sb(256, I32), "ri": sb(512, I32), "rb": sb(512, BF), "nx0": sb(512, BF),
    "win0": sb(NR * WB, BF), "win1": sb(NR * WB, BF), "win2": sb(NR * WB, BF),
    "ll0": sb(NR * P, BF), "ll1": sb(NR * P, BF), "ll2": sb(NR * P, BF),
    "G": sb(4608, BF), "O": sb(4608, BF), "D0": sb(4608, BF), "SG": sb(4096, BF),
    "ones": sb(128, BF), "B1": sb(128, BF), "B": sb(128, BF), "idb": sb(128, BF), "idh": sb(128, F16), "idf": sb(128, F32),
    "id8": sb(128, BF), "idm8": sb(128, BF), "idp": sb(128, F32),
    "E": sb(128, BF), "Z": sb(144, BF), "kneg": sb(128, BF), "kpos": sb(128, BF),
    "high": sb(512, BF), "cb": sb(1040, BF), "cap": sb(512, BF), "dig": sb(512, BF), "dign": sb(512, BF),
    "lo": sb(64, BF), "i8": sb(8, F32), "bc": sb(8, F32), "bcn": sb(8, F32), "Z2": sb(144, BF), "ids": sb(128, BF),
    "pi": sb(8, I32), "pm": sb(8, I32), "pf": sb(8, F32), "i32": sb(32, I32), "vc": sb(32, F32),
    "pa0": sb(32, BF), "pa1": sb(32, BF), "pa2": sb(32, BF), "pb": sb(32, F32), "pc": sb(32, F32), "pos": sb(32, U16),
    "k512": sb(8, F32), "C": sb(8, F32), "cs": sb(8, F32), "nf": sb(8, F32),
    "t1": sb(256, I32), "t2": sb(256, F32), "t3": sb(256, I32), "t4": sb(256, I32), "d1": sb(256, I32), "d2": sb(256, I32),
    "L": sb(256, F32), "off": sb(256, U16), "ju": sb(256, U16), "jh": sb(256, F16), "tm": sb(3 * 256, F16),
    "idx": sb(256, U16), "h": sb(256, F32), "ub": sb(256, BF), "Lf": sb(256, F32), "yxs": sb(512, F32), "ynbs": sb(256, F32),
}
for _n in ("pTa", "pTb", "pW", "pF", "pI", "pSa", "pSb", "pSc"):
    SCRATCH[_n] = ("psum", [128, 512], F32)
SEMAPHORES = ["cV", "cS", "cP", "cG", "ldxa", "ldxb", "ldn", "ldd", "ldr", "sty", "stn0", "stn1", "stn2", "sent",
              "aw0", "aw1", "aw2", "al0", "al1", "al2"]

CA = [12, 12, 12]
SLA = (0, 128, 192, 256)

START = """nxa idb ta ia0 Da i8 i32 pm ia3 idp kpos nxb pm1 rb pf tb lo Z ib0 ia1 idf kneg t1 ib1 t4 E Db ib2 pw ev ib4 g8a t2 idm8 vc bcn ib3 g8b wc bc t3 Z2 pa L pb Dc idh pc dign d1 pos dig k512 id8 off d2 ids scat res"""
DAY = """b5V c4S ^w2 ^m2 a1S C a5S f4 c0V nf ^n2 cs a2V ^o2 ju c3S f3 c6V t0 c7S t2 b1S t1 jh f0 ua b2S p1 p0 x1 s5S ub f1 ta l1 ia0 f5 x0 f6 ia3 s4S tb ia1 ib0 f2 f7 p2 g8b ib1 ib2 ib4 x2 h0 pw l2 ib3 g8a s13S h2 pa h1 w1 l0 pb pc m1 s0S pos w0 n1 s7S scat m0 s6S o1 n0 o0"""
LAST = """^w2 C c4S c5V cs nf ^m2 f4 c2S ju ^n2 c3S c0V c1S t1 f5 jh f2 f3 ^o2 c6S t2 t0 p0 p1 f0 f1 c7V x0 p2 blk s3V s12S s0V x1 f7 s45S x2 u f6 l2 l0 s7S s6V plain l1 h0 h1 w0 w1 h2 m0 m1 yx w2 n0 n1 m2 n2"""


def rank_program(g, core, T, topo):
    q = T.rank_of(core)
    if q is None:
        return
    V, S, PE, SY = g.vector, g.scalar, g.tensor, g.sync
    Q = {"V": V, "S": S, "P": PE, "G": g, "Y": SY}
    count = {}
    known = {k: {} for k in Q}
    writer, readers = {}, {}

    def need(e, ev):
        sem, val, clock = ev
        if known[e].get(sem, 0) < val:
            Q[e].wait_ge(T.sem[sem], val)
            known[e][sem] = val
        for s, v in clock.items():
            if known[e].get(s, 0) < v:
                known[e][s] = v

    def op(e, fn, r=(), w=(), x=(), sem=None):
        evs = [writer[k][1] for k in tuple(r) + tuple(w) if k in writer]
        evs += [ev for k in w for qe, ev in readers.get(k, [])]
        evs += [writer[k][1] for k in x if k in writer and writer[k][0] != e]
        for ev in sorted(evs, key=lambda z: -z[1]):
            need(e, ev)
        ins = fn()
        inc = 1 if sem is None else 16
        sem, who = ("c" + e, e) if sem is None else (sem, "dma")
        count[sem] = count.get(sem, 0) + inc
        ins.then_inc(T.sem[sem], inc)
        ev = (sem, count[sem], dict(known[e]))
        for k in r:
            readers.setdefault(k, []).append((who, ev))
        for k in tuple(w) + tuple(x):
            writer[k] = (who, ev)
            readers[k] = []

    def ts(out, in0, s1, s2, o0, o1=None):
        if o1 is None:
            return V.tensor_scalar(out, in0, s1, None, o0)
        return V.tensor_scalar(out, in0, s1, s2, o0, o1)

    def group(mms, start=True, stop=True):
        ins = None
        for i, (o, l, rr) in enumerate(mms):
            ins = PE.matmul(o, l, rr, start and i == 0, stop and i == len(mms) - 1)
        return ins

    near = [c for c in T.cores if topo.die(c) == topo.die(core)]
    far = [c for c in T.cores if topo.die(c) != topo.die(core)]
    me = near.index(core)
    others = []
    for i in range(max(len(near), len(far))):
        others += far[(me + i) % len(far):][:1] if i < len(far) else []
        others += near[(me + i + 1) % len(near):][:1] if i + 1 < len(near) else []
    emask = -1
    for c in others:
        emask &= topo.mask(core, c)
    neng = bin(emask).count("1")
    sent = {"sent": 0}

    def allgather(ap, r, sem, name):
        for k in r:
            need("G", writer[k][1])
        ids = [DstId(rid=topo.addr(c)[0], pnc=topo.addr(c)[1]) for c in others]
        g.remote_dma_fused([RemoteDMATransfer(dst_ids=ids, dma_engine_mask=emask, remote_sem=T.sem[sem], src=ap,
                                              dsts=[ap for _ in others])], local_sem=T.sem.sent)
        sent["sent"] += neng
        sent[sem] = sent.get(sem, 0) + neng * (NR - 1)
        writer[name] = ("dma", (sem, sent[sem], {}))

    win = [T.win0, T.win1, T.win2]
    ll = [T.ll0, T.ll1, T.ll2]
    dd = [T.d0, T.d1, T.d2]
    pa = [T.pa0, T.pa1, T.pa2]
    Wr = [T.Z[:, 15 - r:143 - r] for r in range(16)]
    Wd = [T.Z2[:, 15 - r:143 - r] for r in range(16)]
    LN = ["L0", "L1", "L2"]
    banks = ["pSa", "pSb", "pSc"]
    pieces = [(banks[i], SLA[i], SLA[i + 1], T[banks[i]][:, 0:SLA[i + 1] - SLA[i]]) for i in range(3)]

    def vop(fn, **kw):
        return lambda: op("V", fn, **kw)

    def pop(fn, **kw):
        return lambda: op("P", fn, **kw)

    def fill(name, n, value):
        return lambda: op("G", lambda: g.iota(T[name][:], [[0, n]], value, 0, allow_small_or_imprecise_dtypes=True), w=[name])

    def sending(t, nx):
        va, step = 16 * CA[t], {}
        for h, v0, v1 in (("a", 0, va), ("b", va, P)):
            def part(h=h, v0=v0, v1=v1):
                c, cp, il = T.cb[:, 16 + v0:16 + v1], T.cb[:, 15 + v0:15 + v1], T.cb[:, 528 + v0:528 + v1]
                prev, bank, blk = "c0" if h == "a" else "cqa", "pT" + h, "blk%d%s" % (t, h)
                step["t" + h] = pop(lambda: PE.matmul(T[bank][:, 0:v1 - v0], T.B[:], nx(v0, v1), True, True), r=["B", "nx" + h], x=[bank])
                high, hn = (il, "ill" + h) if v1 <= CAP else (T.high[:, v0:v1], "high" + h)
                step["i%s0" % h] = vop(lambda: ts(high, T[bank][:, 0:v1 - v0], -TH + 0.5, None, A.is_le), w=[hn], x=[bank])
                step["i%s1" % h] = vop(lambda: V.tensor_tensor_scan(c, high, T.cap[:, v0:v1], T.cb[:, 15 + v0:16 + v0], A.add, A.min),
                                       r=[hn, "cap", prev], w=["cq" + h])
                step["i%s2" % h] = vop(lambda: V.tensor_tensor_scan(il, c, cp, 0.0, A.max, A.subtract), r=["cq" + h, prev], w=["ill" + h])

                def send():
                    op("V", lambda: V.tensor_tensor_scan(win[t][:, WB * q + v0:WB * q + v1], il, nx(v0, v1), 0.0, A.max, A.mult),
                       r=["ill" + h, "nx" + h] + ([] if h == "a" else ["tail%d" % t]), w=[blk])
                    allgather(win[t][:, WB * q + v0:WB * q + (v1 if h == "a" else WB)], [blk], "aw%d" % t, "win%d" % t)
                step["i%s3" % h] = send
            part()
        step["ib4"] = vop(lambda: V.tensor_copy(win[t][:, WB * q + P:WB * (q + 1)], T.cb[:, 520:528]), r=["cqb"], w=["tail%d" % t])
        step["pw"] = pop(lambda: group([(T.pW[:, 0:64], Wr[r], T.cb[:, 16 + r:1040:16]) for r in range(16)]),
                         r=["Z", "cqa", "cqb", "illa", "illb"], x=["pW"])
        step["g8a"] = vop(lambda: ts(T.G[:, 8:9 * va:9], nx(0, va), 8.0, 0.0, A.add, A.min), r=["nxa"], w=["G8a"])
        step["g8b"] = vop(lambda: ts(T.G[:, 9 * va + 8::9], nx(va, P), 8.0, 0.0, A.add, A.min), r=["nxb"], w=["G8b"])
        odd = q % 2
        step["pa"] = vop(lambda: ts(pa[t][:], T.pW[:, 32:64], 512.0 if odd else -512.0, 0.0 if odd else 512.0, A.mult, A.add), w=["pa%d" % t], x=["pW"])
        step["pb"] = vop(lambda: V.tensor_tensor(T.pb[:], pa[t][:], T.vc[:], A.max if odd else A.min), r=["pa%d" % t, "vc"], w=["pb"])
        step["pc"] = vop(lambda: V.tensor_tensor(T.pc[:], T.pb[:], T.pW[:, 0:32], A.subtract), r=["pb"], w=["pc"], x=["pW"])
        step["pos"] = vop(lambda: ts(T.pos[:], T.pc[:], 0.0 if odd else T.cb[:, 527:528], None, A.add), r=["pc", "cqb"], w=["pos"])

        def scatter():
            lb, dig = ll[t][:, P * q:P * (q + 1)], "dig" if t < DAYS - 1 else "dign"
            op("V", lambda: V.tensor_copy(lb.indirect(T.pos[:]), T[dig][:]), r=["pos", dig], w=["lb%d" % t])
            allgather(lb, ["lb%d" % t], "al%d" % t, "ll%d" % t)
        step["scat"] = scatter
        return step

    def nx0(v0, v1):
        return T.nx0[:, v0:v1]

    def nxo(v0, v1):
        return T.O[:, 9 * v0 + 8:9 * v1:9]

    def daily(t):
        last, step = t == DAYS - 1, {}
        ca = CA[min(t + 1, DAYS - 1)]
        wn = ["win%d" % t, "blk%da" % t, "blk%db" % t]
        nf = win[t][:, WB - 1::WB]

        def pick(e, out, src, r, names):
            if e == "V":
                return vop(lambda: V.tensor_copy(out, src), r=r, w=names)
            return lambda: op("S", lambda: S.activation(out, src, AF.Copy), r=r, w=names)

        for k in range(8):
            i = max(i for i in range(3) if SLA[i] <= 32 * k)
            for e in "VS":
                for h, c0, c1, hs in (("a", 0, ca, "a"), ("b", ca, 32, "b"), ("c", 0, 32, "ab")):
                    step["%s%d%s" % (h, k, e)] = pick(e, T.G[:, 144 * c0 + k:144 * c1:9], win[t][:].indirect(T.off[:, 32 * k + c0:32 * k + c1]),
                                                      wn + ["off%d" % i], ["G%s%d" % (x, k) for x in hs])
                for k1 in range(k, 8):
                    step["s%d%s%s" % (k, k1 if k1 > k else "", e)] = pick(
                        e, T.SG[:, 512 * k:512 * k1 + 512], ll[t][:].indirect(T.idx[:, 32 * k:32 * k1 + 32]),
                        ["ll%d" % t, "lb%d" % t] + ["idx%d" % j for j in range(i, 3) if SLA[j] <= 32 * k1], ["SG%d" % j for j in range(k, k1 + 1)])

            def flags(k=k):
                out = T.pF[:, 32 * k:32 * k + 32]
                mm = [(out, Wr[r], T.G[:, 9 * r + k::144]) for r in range(16)] + [(out, T.ids[:], pa[t][:])]
                op("P", lambda: group(mm), r=["Z", "ids", "pa%d" % t, "Ga%d" % k, "Gb%d" % k], w=["F%d" % k], x=["pF"])
            step["f%d" % k] = flags
        for name, v0, v1, hs in (("ua", 0, 16 * ca, "a"), ("ub", 16 * ca, P, "b"), ("u", 0, P, "ab")):
            step[name] = vop(lambda v0=v0, v1=v1: V.tensor_tensor_scan(T.O[:, 9 * v0:9 * v1], T.D0[:, 9 * v0:9 * v1], T.G[:, 9 * v0:9 * v1], 0.0, A.add, A.min),
                             r=["G%s%d" % (h, k) for k in range(8) for h in hs] + ["G8a", "G8b", "D0a"], w=["nx" + h for h in hs])
        step["C"] = vop(lambda: V.tensor_tensor_scan(T.C[:], T.k512[:], nf, 0.0, A.add, A.subtract), r=wn + ["k512"], w=["C"])
        step["cs"] = vop(lambda: ts(T.cs[:, 0:1], T.C[:, 7:8], 1.0 / 2048, None, A.mult), r=["C"], w=["cs"])
        step["ju"] = vop(lambda: ts(T.ju[:], dd[t][:], T.cs[:, 0:1], -0.5 + 2.0 ** -12, A.mult, A.add), r=["cs", "d%d" % t], w=["ju"])
        step["jh"] = vop(lambda: ts(T.jh[:], T.ju[:], nf[:, 0:1], -2048.0, A.add, A.add), r=["ju"] + wn, w=["jh"])
        for i in range(3):
            step["t%d" % i] = vop(lambda i=i: ts(T.tm[:, 256 * i:256 * (i + 1)], T.ju[:], T.C[:, 2 * i + 1:2 * i + 2], T.nf[:, i:i + 1], A.is_ge, A.mult),
                                  r=["ju", "C", "nf"], w=["tm%d" % i])
        step["nf"] = vop(lambda: V.tensor_tensor(T.nf[:, 0:3], nf[:, 1:6:2], nf[:, 2:7:2], A.add), r=wn, w=["nf"])
        for i, (bank, c0, c1, out) in enumerate(pieces):
            def piece(i=i, bank=bank, c0=c0, c1=c1, out=out):
                ks = range(c0 // 32, c1 // 32)
                mm = [(out, T.idh[:], T.jh[:, c0:c1])] + [(out, T.idh[:], T.tm[:, 256 * j + c0:256 * j + c1]) for j in range(3)]
                step["p%d" % i] = pop(lambda: group(mm), r=["jh", "idh"] + ["tm%d" % j for j in range(3)], x=[bank])
                step["x%d" % i] = vop(lambda: ts(T.idx[:, c0:c1], out, 2048.0, None, A.add), w=["idx%d" % i], x=[bank])
                ml = [(out, T.idf[:], T.L[:, c0:c1])]
                if last:
                    ml += [(out, T.idb[:], T.kneg[:, 0:c1 - c0]), (out, T.id8[:], T.ub[:, c0:c1])]
                step["l%d" % i] = pop(lambda: group(ml, stop=False), r=[LN[i], "idf", "kneg", "id8", "ub"], x=[bank])
                step["w%d" % i] = pop(lambda: group([(out, Wd[r], T.SG[:, 16 * c0 + r:16 * c1:16]) for r in range(16)], start=False),
                                      r=["Z2"] + ["SG%d" % k for k in ks], x=[bank])
                step["h%d" % i] = vop(lambda: ts(T.h[:, c0:c1], T.pF[:, c0:c1], -30.0 if q % 2 else -542.0, None, A.is_lt), r=["F%d" % k for k in ks], w=["h%d" % i], x=["pF"])
                pw = T.pI[:, 256 + c0:256 + c1]
                if last:
                    step["m%d" % i] = vop(lambda: V.tensor_tensor(T.Lf[:, c0:c1], out, T.h[:, c0:c1], A.mult), r=["h%d" % i], w=["dl%d" % i], x=[bank])

                    def store():
                        op("V", lambda: V.tensor_tensor(T.ynbs[:, c0:c1], T.pI[:, c0:c1], T.Lf[:, c0:c1], A.add), r=["dl%d" % i], w=["yn%d" % i], x=["pI"])
                        op("Y", lambda: SY.dma_start(T.ynb[:, c0:c1], T.ynbs[:, c0:c1]), r=["yn%d" % i], sem="stn%d" % i)
                    step["n%d" % i] = store
                else:
                    step["m%d" % i] = vop(lambda: V.tensor_tensor(pw, out, T.h[:, c0:c1], A.mult), r=["h%d" % i], w=["dl%d" % i], x=[bank, "pI"])
                    step["n%d" % i] = vop(lambda: V.tensor_tensor(T.L[:, c0:c1], pw, T.L[:, c0:c1], A.add), r=["dl%d" % i], w=[LN[i]], x=["pI"])
                    step["o%d" % i] = vop(lambda: V.tensor_copy(T.off[:, c0:c1], T.L[:, c0:c1]), r=[LN[i]], w=["off%d" % i])
            piece()
        step["blk"] = vop(lambda: ts(T.ub[:], T.L[:], 1.0 / WB, UB - 0.492, A.mult, A.add), r=LN, w=["ub"])

        def plain():
            for c0 in (0, 128):
                out = T.pI[:, c0:128 + c0]
                op("P", lambda: group([(out, T.idp[:], T.L[:, c0:c0 + 128]), (out, T.idm8[:], T.ub[:, c0:c0 + 128]), (out, T.idb[:], T.kpos[:])]),
                   r=LN + ["idp", "idm8", "ub", "kpos"], x=["pI"])
        step["plain"] = plain

        def loads():
            op("S", lambda: S.activation(T.yxs[:], T.O[:, 8::9], AF.Copy, scale=-1.0), r=["nxa", "nxb"], w=["yxs"])
            op("Y", lambda: SY.dma_start(T.yx[:], T.yxs[:]), r=["yxs"], sem="sty")
        step["yx"] = loads
        if not last:
            step.update(sending(t + 1, nxo))
        return step

    va = 16 * CA[0]
    op("Y", lambda: SY.dma_start(T.xi[:, 0:va], T.x0[:, 0:va]), w=["xia"], sem="ldxa")
    op("S", lambda: S.dma_start(T.xi[:, va:P], T.x0[:, va:P]), w=["xib"], sem="ldxb")
    op("Y", lambda: SY.dma_start(T.nbi[:], T.nb[:]), w=["nbi"], sem="ldn")
    op("S", lambda: S.dma_start(T.ri[0:8, :], T.res[:]), w=["ri"], sem="ldr")
    op("Y", lambda: SY.dma_start(T.d0[:], T.dice[:]), w=["d0"], sem="ldd")
    op("V", lambda: V.memset(T.ones[:], 1.0), w=["ones"])
    op("V", lambda: V.memset(T.D0[:, 0:576], 0.0), w=["D0a"])
    op("V", lambda: V.memset(T.cap[:], float(CAP)), w=["cap"])
    op("V", lambda: V.memset(T.cb[:, 0:16], 0.0), w=["c0"])
    op("V", lambda: V.memset(T.D0[:, 0:576:9], 512.0), r=["D0a"], w=["D0a"])
    op("V", lambda: V.memset(T.Z[:], 0.0), w=["Z"])
    op("V", lambda: V.memset(T.Z2[:], 0.0), w=["Z2"])
    op("G", lambda: g.affine_select(T.B1[:], T.ones[:], [[-16, 8], [0, 16]], A.is_ge, 0.0, 0, 1), r=["ones"], w=["B1"])
    op("G", lambda: g.affine_select(T.B[:], T.B1[:], [[16, 8], [0, 16]], A.is_ge, 0.0, 15, -1), r=["B1"], w=["B"])
    op("G", lambda: g.iota(T.pi[:], [[0, 8]], 0, 1), w=["pi"])

    def ramp(name, n, step):
        return lambda: op("G", lambda: g.iota(T[name][:], [[step, n]], 0, 0, allow_small_or_imprecise_dtypes=True), w=[name])

    def double(n):
        return lambda: op("S", lambda: S.activation(T.D0[:, n:2 * n], T.D0[:, 0:n], AF.Copy), r=["D0a"], w=["D0a"])

    def scaled(name, f):
        return lambda: op("S", lambda: S.activation(T[name][:], T.idb[:], AF.Copy, scale=f), r=["idb"], w=[name])

    def digits(name, bias):
        def run():
            for c in range(8):
                op("S", lambda: S.activation(T[name][:, 64 * c:64 * c + 64], T.lo[:], AF.Identity, bias=T[bias][:, c:c + 1], scale=T.pf[:, 1:2]),
                   r=["lo", bias, "pf0"], w=[name + str(c)] if c < 7 else [name])
        return run

    def resist():
        op("P", lambda: PE.matmul(T.pTa[:], T.E[0:8, :], T.rb[0:8, :], True, True), r=["E", "rb"], x=["pTa"])
        op("S", lambda: S.activation(T.D0[:, 8::9], T.pTa[:], AF.Copy), r=["D0a"], w=["D0a"], x=["pTa"])

    first = sending(0, nx0)
    first.update({
        "nxa": vop(lambda: ts(T.nx0[:, 0:va], T.xi[:, 0:va], -1.0, None, A.mult), r=["xia"], w=["nxa"]),
        "nxb": vop(lambda: ts(T.nx0[:, va:P], T.xi[:, va:P], -1.0, None, A.mult), r=["xib"], w=["nxb"]),
        "pm": vop(lambda: ts(T.pm[:, 0:1], T.pi[:, 0:1], 15, None, A.bitwise_and), r=["pi"], w=["pm0"]),
        "Z": vop(lambda: ts(T.Z[:, 15:128:16], T.B[:, 0:128:16], 1.0 / 16, None, A.mult), r=["B", "Z"], w=["Z"]),
        "pm1": vop(lambda: ts(T.pm[:, 1:2], T.pi[:, 1:2], 1, None, A.bitwise_and), r=["pi"], w=["pm1"]),
        "pf": vop(lambda: V.tensor_copy(T.pf[:, 0:2], T.pm[:, 0:2]), r=["pm0", "pm1"], w=["pf0"]),
        "ev": vop(lambda: ts(T.pf[:, 2:3], T.pm[:, 1:2], -1.0, 1.0, A.mult, A.add), r=["pm1"], w=["ev"]),
        "wc": vop(lambda: ts(T.pf[:, 3:4], T.pm[:, 1:2], 1.0 / 8 - 8, 8.0, A.mult, A.add), r=["pm1"], w=["wc"]),
        "Z2": vop(lambda: ts(T.Z2[:, 15:128:16], T.B[:, 0:128:16], T.pf[:, 3:4], None, A.mult), r=["B", "Z2", "wc"], w=["Z2"]),
        "bc": vop(lambda: ts(T.bc[:], T.i8[:], T.pf[:, 2:3], 8.0 * q, A.mult, A.add), r=["i8", "ev"], w=["bc"]),
        "bcn": vop(lambda: ts(T.bcn[:], T.i8[:], 8.0 * q, T.pf[:, 2:3], A.add, A.mult), r=["i8", "ev"], w=["bcn"]),
        "dig": digits("dig", "bc"), "dign": digits("dign", "bcn"),
        "i32": ramp("i32", 32, 16), "i8": ramp("i8", 8, 1), "lo": ramp("lo", 64, 1),
        "idb": lambda: op("G", lambda: g.affine_select(T.idb[:], T.ones[:], [[-1, 128]], A.is_equal, 0.0, 0, 1), r=["ones"], w=["idb"]),
        "E": lambda: op("G", lambda: g.affine_select(T.E[0:8, :], T.ones[0:8, :], [[-1, 8], [0, 16]], A.is_equal, 0.0, 0, 1), r=["ones"], w=["E"]),
        "Da": double(576), "Db": double(1152), "Dc": double(2304),
        "idf": scaled("idf", -1.0), "id8": scaled("id8", 8.0), "idm8": scaled("idm8", -8.0), "idp": scaled("idp", 1.0),
        "ids": scaled("ids", 1.0 if q % 2 else -1.0),
        "vc": vop(lambda: ts(T.vc[:], T.i32[:], T.pf[:, 0:1], None, A.add), r=["pf0", "i32"], w=["vc"]),
        "idh": vop(lambda: V.tensor_copy(T.idh[:], T.idb[:]), r=["idb"], w=["idh"]),
        "k512": fill("k512", 8, P), "kneg": fill("kneg", 128, -8 * UB), "kpos": fill("kpos", 128, 8 * UB),
        "rb": vop(lambda: V.tensor_copy(T.rb[0:8, :], T.ri[0:8, :]), r=["ri"], w=["rb"]),
        "res": resist,
        "t1": vop(lambda: ts(T.t1[:], T.nbi[:], 3584, None, A.bitwise_and), r=["nbi"], w=["t1"]),
        "t2": vop(lambda: ts(T.t2[:], T.t1[:], 1.0 / 64, None, A.mult), r=["t1"], w=["t2"]),
        "L": vop(lambda: V.tensor_tensor(T.L[:], T.t2[:], T.nbi[:], A.add), r=["t2", "nbi"], w=LN),
        "off": vop(lambda: V.tensor_copy(T.off[:], T.L[:]), r=LN, w=["off0", "off1", "off2"]),
        "t3": vop(lambda: ts(T.t3[:], T.d0[:], float(STEP), None, A.add), r=["d0"], w=["t3"]),
        "d1": vop(lambda: ts(T.d1[:], T.t3[:], 2047, None, A.bitwise_and), r=["t3"], w=["d1"]),
        "t4": vop(lambda: ts(T.t4[:], T.d0[:], float(2 * STEP), None, A.add), r=["d0"], w=["t4"]),
        "d2": vop(lambda: ts(T.d2[:], T.t4[:], 2047, None, A.bitwise_and), r=["t4"], w=["d2"]),
    })
    before = {}
    for steps, order in ((first, START), (daily(0), DAY), (daily(1), DAY), (daily(2), LAST)):
        for name in order.split():
            if name[0] != "^":
                steps[name]()
            elif name[1:] in before:
                before[name[1:]]()
        before = steps if steps is not first else {}

    g.wait_ge(T.sem.sent, sent["sent"])
    for s in ("cV", "cS", "cP", "cG", "sty", "stn0", "stn1", "stn2"):
        SY.wait_ge(T.sem[s], count[s])
